import numpy as np, ml_dtypes
CORES = [16,18,20,22]
N = 4
import mx_ref
BF = ml_dtypes.bfloat16
def gentries(a):
    return np.ascontiguousarray(a.reshape(8, 16, -1).transpose(0, 2, 1)).reshape(8, -1)
def gtable(e):
    e = np.asarray(e); return np.ascontiguousarray(e.reshape(8, -1, 16).transpose(0, 2, 1)).reshape(128, -1).astype(np.int32)
def gcols(t, e):
    v = np.concatenate([t.reshape(8, 16, -1, 4), np.zeros((8, 16, 1, 4), BF)], axis=2)
    return np.ascontiguousarray(np.stack([v[g][:, e[g]] for g in range(8)])).reshape(128, -1)
def tile(rs):
    return np.stack(rs, axis=2).reshape(128, -1).astype(BF)
def pick(q, e):
    c = np.concatenate([q[0].reshape(128, -1, 4), np.zeros((128, 1, 4), np.uint8)], axis=1); s = np.concatenate([q[1], np.ones((16, 1), np.uint8)], axis=1)
    return (np.ascontiguousarray(c[:, e].reshape(128, -1)), np.ascontiguousarray(s[:, e]))
def join(*qs):
    return (np.concatenate([q[0] for q in qs], axis=1), np.concatenate([q[1] for q in qs], axis=1))
def put(q, e, v):
    c, s = q[0].reshape(128, -1, 4).copy(), q[1].copy(); c[:, e] = v[0].reshape(128, -1, 4); s[:, e] = v[1]
    return (c.reshape(128, -1), s)
def pk(c, s):
    return (np.ascontiguousarray(c), mx_ref.live(s))
def emit(q):
    return q[0], q[1]
def packed(v, rng):
    q = [mx_ref.quantize(np.ascontiguousarray(v[r])) for r in range(N)]
    return np.stack([a for a, b in q]), np.stack([mx_ref.plane(b, rng) for a, b in q])
def values_of_codes():
    e, c = np.zeros((128, 128, 4), np.float32), np.zeros((128, 2, 4), np.uint8)
    e[np.arange(128), np.arange(128), 0] = 1
    c[:127, :, 0] = np.arange(256).reshape(2, 128).T[:127]
    return mx_ref.matmul(mx_ref.quantize(e.reshape(128, 512).astype(BF)), (c.reshape(128, 8), np.full((16, 2), 127, np.uint8))).T.reshape(-1).astype(np.float64)
CODE_VALUE, SCALE_VALUE = values_of_codes(), 2.0 ** (np.arange(256) - 127.0)
def decode(q):
    return (CODE_VALUE[q[0]].reshape(16, 8, -1, 4) * SCALE_VALUE[q[1]][:, None, :, None] + 0.0).reshape(128, -1).astype(np.float32)
def f(rng, *shape):
    return mx_ref.flush((rng.standard_normal(shape, dtype=np.float32) * np.exp2(rng.integers(-2, 3, shape[:-1] + (1,)))).astype(BF))
def wide(rng, *shape, cols=0):
    v = rng.standard_normal(shape, dtype=np.float32) * np.exp2(rng.integers(-12, 13, shape)).astype(np.float32)
    if cols: v *= np.repeat(np.exp2(rng.integers(-cols, cols + 1, shape[:-2] + (1, shape[-1] // 4))) * (rng.random(shape[:-2] + (1, shape[-1] // 4)) > 0.0625), 4, axis=-1).astype(np.float32)
    return mx_ref.flush(v.astype(BF))
C, DOUBLINGS = 384, 9
STEP = [1, 2, 3]
def numbers_of(rng):
    return {"x": np.array(f(rng, N, 128, 4 * C)), "u": np.array(f(rng, N, 128, 512)), "v": np.array(f(rng, N, 128, 512))}
def links(rng, far=False):
    l = rng.permuted(np.tile(np.arange(C), (N, 8, 2, 1)), axis=3)
    if far:
        for r in range(N):
            for i, g in enumerate(rng.permutation(8)[:6]):
                o = rng.permutation(C)
                l[r, g, 0, o] = np.append(o[1:], o[[0, C - 1, C // 2][i % 3]])
                if i < 3: l[r, g, 1] = l[r, g, 0]
    return l
def stored(l):
    return {"la": np.stack([gtable(l[r, :, 0]) for r in range(N)]), "lb": np.stack([gtable(l[r, :, 1]) for r in range(N)])}
def layers(rng, still=[]):
    w = np.array(f(rng, N, 128, 2048)).reshape(N, 8, 16, 4, 8, 16, 4)
    for i in still:
        w[:, :, i] = 0
        w[:, :, :, :, :, i] = 0
    return w
def weights(rng, w):
    c, p = packed(np.ascontiguousarray(w).reshape(N, 128, 2048), rng)
    return {"wc": c, "ws": p}
def setup_inputs(rng):
    return {**numbers_of(rng), **stored(links(rng)), **weights(rng, layers(rng))}
def setup_inputs_ties(rng):
    d = numbers_of(rng)
    o = rng.permutation(N)
    k = rng.integers(-2, 3, (N, 8, C))
    k[o[1]] = -rng.integers(1, 5, (8, C))
    far = rng.permutation(8)
    k[o[2], far[:4]] = 1
    k[o[3], rng.permutation(8)[:4]] = -1
    l = links(rng, True)
    way = rng.permutation(C)
    way[-2:] = np.sort(way[-2:])
    for g, end, top in ((far[4], way[-1], way[-1]), (far[5], way[0], 0)):
        l[o[2], g, 0, way] = np.append(way[1:], end)
        l[o[2], g, 1] = np.arange(C)
        k[o[2], g] = 1
        k[o[2], g, top] = 2
    x = d["x"].reshape(N, 8, 16, C, 4)
    x[:, :, 0] = 0
    x[:, :, 0, :, 0] = k.astype(np.float32).astype(BF)
    u = d["u"].reshape(N, 128, 128, 4)
    u[:, :, ::16] = 0
    for r in range(N):
        for h in range(0, 128, 16): u[r, h, h, 0] = 0.0 if r == o[0] else 1.0
    return {"x": x.reshape(N, 128, 4 * C), "u": u.reshape(N, 128, 512), "v": d["v"], **stored(l), **weights(rng, layers(rng, [0]))}
def setup_inputs_near(rng):
    d = numbers_of(rng)
    x = d["x"].astype(np.float32).reshape(N, 8, 16, C, 4)
    x[:, :, 0] = 0
    x[:, :, 8:] = 0
    u = d["u"].reshape(N, 128, 128, 4)
    u[:, :, ::16] = 0
    w = layers(rng, [0, 8, 9, 10, 11, 12, 13, 14, 15])
    o = rng.permutation(N) % 4
    for r in range(N):
        s = rng.integers(0, 16, (8, C))
        digits = ((s[:, :, None] >> np.arange(4)) & 1) * np.exp2(np.arange(4) - 23.0)
        if o[r] < 3: x[r, :, 12, :, 0] = rng.choice([-1.0, 1.0], (8, C)) * 2.0 ** -20
        if o[r] < 2:
            x[r, :, 0, :, 0] = np.where(rng.permutation(8) < 4, -1.0, 1.0)[:, None]
            x[r, :, 8] = digits
            x[r, :, 11, :, 0] = 2.0 ** -10
        elif o[r] == 2: x[r, :, 8] = digits * rng.choice([-1.0, 1.0], (8, C, 1))
        else:
            e = rng.integers(-1, 2, (8, C)) * 2.0 ** -30
            x[r, :, 8, :, 0] = 1.25 * e
            x[r, :, 9, :, 0] = -1.125 * e
            x[r, :, 15, :, 0] = 2.0 ** -30
            for g in range(8):
                w[r, g, 12, 0, g, 10, 0] = 2.0 ** -18
                w[r, g, 14, 0, g, 10, 0] = 2.0 ** -8
        at = [0, C - 1, int(rng.integers(C)), int(rng.integers(C))]
        for g, j in zip(rng.permutation(8)[:4], at): x[r, g, 0, j, 0] = 2.0 ** 29 * rng.choice([-1.0, 1.0])
        k = 1.0 if o[r] == 0 else 2.0 ** -30
        for h in range(0, 128, 16):
            u[r, h, h, 0] = k if o[r] < 2 else 1.0
            if o[r] < 2: u[r, h + 11, h, 0] = k
            if o[r] < 3: u[r, h + 8, h] = k
            else:
                u[r, h + 8, h, 0] = k
                u[r, h + 9, h, 0] = 1.125 * k
                u[r, h + 10, h, 0] = k
    return {"x": x.reshape(N, 128, 4 * C).astype(BF), "u": u.reshape(N, 128, 512), "v": d["v"], **stored(links(rng, True)), **weights(rng, w)}
def setup_inputs_odd(rng):
    d = numbers_of(rng)
    x = (1.0 + (2 * rng.integers(0, 64, (N, 16, 8, C, 4)) + 1) * 2.0 ** -7) * np.exp2(-rng.integers(0, 7, (N, 16, 8, C, 4)).astype(np.float64)) * rng.choice([-1.0, 1.0], (N, 16, 8, C, 4))
    x[:, :, 0, :, 0] = np.where(rng.random((N, 16, C)) < 0.25, 1.875, 1.96875) * 2.0 ** 8
    x[:, ::2, 1, :, 0] = rng.choice([-1.0, 1.0], (N, 8, C)) * (8 + rng.integers(0, 2, (N, 8, C))) * 2.0 ** -8
    u = d["u"].reshape(N, 16, 8, 128, 4)
    u[:, :, :, ::16] = 0
    for g in range(8): u[:, 2 * g, 1, 16 * g, 0] = 1.0
    return {"x": x.astype(np.float32).reshape(N, 128, 4 * C).astype(BF), "u": u.reshape(N, 128, 512), "v": d["v"], **stored(links(rng)), **weights(rng, layers(rng, [0, 8]))}
def setup_inputs_ends(rng):
    d = numbers_of(rng)
    o, e = rng.permutation(N) % 4, rng.permutation(N) % 4
    m = int(rng.integers(8))
    l = links(rng, True)
    small = -(1.0 + 0.125 * rng.integers(0, 8, (N, 8, 16, C, 4)))
    x = -(0.88 + 0.08 * rng.random((N, 8, 16, C, 4))) * 2.0 ** 30
    x[o == 1] *= rng.choice([-1.0, 1.0], (N, 1, 1, C, 1))[o == 1]
    x[o == 2] = small[o == 2] * 2.0 ** -30
    x[o == 3] = d["x"].astype(np.float32).reshape(N, 8, 16, C, 4)[o == 3][:, :, :, :1]
    x[:, m] = small[:, m] * 2.0 ** -20
    u = d["u"].astype(np.float32).reshape(N, 8, 16, 128, 4)
    v = rng.choice([-1.0, 1.0], (N, 128, 512)) * np.where(o < 2, 2.0 ** 30, 2.0 ** -30)[:, None, None]
    w = np.zeros((N, 128, 4, 128, 4), np.float32)
    i = np.arange(128)
    for r in range(N):
        h = rng.permutation(8)
        c = np.where(h < 2, 0.0, h % 2 * 2.0 - 1.0)[:, None]
        if o[r] < 2: u[r, :, :, ::16] = c * (0.9 + 0.1 * rng.random((8, 16, 8, 4))) * 2.0 ** 30
        if o[r] == 2: u[r, :, :, ::16] = c * (1.0 + 0.125 * rng.integers(0, 8, (8, 16, 8, 4))) * 2.0 ** -30
        if o[r] == 3: u[r, :, :, ::16] *= np.abs(c).astype(np.float32)
        k = np.zeros(8)
        if o[r] < 2: k = rng.choice([-1.0, 1.0], 8) * np.array([0.75, 0.5, 2.0 ** -8])[rng.permutation(8) % 3]
        k[m] = 2.0 ** 8
        for b in range(4): w[r, i, b, i, b] = k[i // 16]
        if e[r] < 2:
            l[r, :, e[r]] = C - 1
            l[r, :, 1 - e[r]] = 0
        if e[r] == 2: l[r] = rng.integers(0, C, (8, 2, C))
    u[:, m, :, ::16] = 0
    return {"x": x.astype(np.float32).reshape(N, 128, 4 * C).astype(BF), "u": u.reshape(N, 128, 512).astype(BF), "v": v.astype(np.float32).astype(BF), **stored(l), **weights(rng, w.astype(BF))}
def setup_inputs_spread(rng):
    d = setup_inputs(rng)
    d["x"] = wide(rng, N, 128, 4 * C, cols=6)
    return d
def check_inputs(d):
    b = []
    for k in ("x", "u", "v"):
        a = np.abs(d[k].astype(np.float32))
        if not (np.isfinite(a).all() and ((a == 0) | (a >= 2.0 ** -30) & (a <= 2.0 ** 30)).all()): b.append("a value of " + k)
    for k in ("la", "lb"):
        if not ((d[k] >= 0) & (d[k] < C)).all(): b.append("an entry of " + k)
    none, least, most = [emit(mx_ref.quantize(np.full((128, 16), k, np.float32).astype(BF)))[1][0, 0] for k in (0.0, 2.0 ** -8, 2.0 ** 8)]
    for r in range(N):
        if ((d["wc"][r] == 0x7F) | (d["wc"][r] == 0xFF)).any(): b.append("wc: a code that is no number")
        s = mx_ref.live(d["ws"][r])
        if ((s != none) & ((s < least) | (s > most))).any(): b.append("ws: a scale out of range")
        if (((d["wc"][r].reshape(16, 8, 512, 4) & 0x7F) != 0) & (s == none)[:, None, :, None]).any(): b.append("wc: a code other than zero under the scale of zeros")
    return b
def look(t, e):
    return np.take_along_axis(t, e, axis=1)
def leaders(p):
    low, at = np.tile(np.arange(C), (8, 1)), p
    for k in range(DOUBLINGS):
        low = np.minimum(low, look(low, at))
        at = look(at, at)
    return look(low, at)
def reference(x, u, v, la, lb, wc, ws):
    qu = [mx_ref.quantize(u[r]) for r in range(N)]
    lay = [pk(wc[r], ws[r]) for r in range(N)]
    l0, l1 = [gentries(la[r]) for r in range(N)], [gentries(lb[r]) for r in range(N)]
    now = [x[r] for r in range(N)]
    for step in STEP:
        own, torn, sent = [], [], []
        for r in range(N):
            q = mx_ref.quantize(now[r])
            s = mx_ref.matmul(qu[r], q)[::16] + np.float32(0.0)
            p = np.where(s < 0, l1[r], l0[r])
            lead = leaders(p)
            e = np.where(lead == np.arange(C), lead, p)
            own.append(decode(q).astype(BF))
            torn.append(e)
            z = own[r]
            for k in range(3):
                z = ((z.astype(np.float32) + gcols(z, e).astype(np.float32)) * np.float32(0.5)).astype(BF)
                e = look(e, e)
            sent.append(mx_ref.quantize(z))
            change = look(s, lead) > s
            l0[r], l1[r] = np.where(change, l1[r], l0[r]), np.where(change, l0[r], l1[r])
        for r in range(N):
            z = sent[(r - step) % N]
            h = tile([mx_ref.matmul(pick(lay[r], np.arange(128 * b, 128 * b + 128)), z) * np.float32(0.03125) for b in range(4)])
            now[r] = (own[r].astype(np.float32) + gcols(h, torn[r]).astype(np.float32)).astype(BF)
    y, ls = np.zeros((N, 128, C), np.float32), np.zeros((N, 8, 2 * C), np.float32)
    oc, osc = np.zeros((N, 128, 4 * C), np.uint8), np.zeros((N, 16, C), np.uint8)
    for r in range(N):
        q = mx_ref.quantize(now[r])
        y[r] = mx_ref.matmul(mx_ref.quantize(v[r]), q)
        ls[r] = np.concatenate([l0[r], l1[r]], axis=1)
        oc[r], osc[r] = emit(q)
    return {"y": y, "ls": ls, "oc": oc, "osc": osc}

@@ -1,0 +1,464 @@
+from concourse.bass import DstId, RemoteDMATransfer
+from concourse.mybir import dt, AluOpType, ActivationFunctionType
+
+C = 384
+HALF = C // 2
+STEPS = [1, 2, 3]
+KT = C // 16
+TWIN = 128
+ROWS = 34
+SLOTS = 14
+TABS = 20
+BIG, LIFT, MID = 2048.0, 512.0, 192.0
+
+SCRATCH = {
+    "ut": ("sbuf", [128, 512], "bfloat16"), "qu": ("sbuf", [128, 128], "float8_e4m3fn_x4"), "qus": ("sbuf", [128, 128], "uint8"),
+    "qr": ("sbuf", [128, 128], "float8_e4m3fn_x4"), "qrs": ("sbuf", [128, 128], "uint8"),
+    "vt": ("sbuf", [128, 512], "bfloat16"), "qv": ("sbuf", [128, 128], "float8_e4m3fn_x4"), "qvs": ("sbuf", [128, 128], "uint8"),
+    "wq": ("sbuf", [128, 512], "float8_e4m3fn_x4"), "wp": ("sbuf", [128, 512], "uint8"),
+    "ones": ("sbuf", [128, 528], "bfloat16"), "et": ("sbuf", [128, 528], "bfloat16"),
+    "qe": ("sbuf", [128, 512], "float8_e4m3fn_x4"), "qes": ("sbuf", [128, 512], "uint8"),
+    "lai": ("sbuf", [128, KT], "int32"), "lbi": ("sbuf", [128, KT], "int32"),
+    "im": ("sbuf", [128, 16], "int32"), "im2": ("sbuf", [128, 16], "int32"), "ma": ("sbuf", [128, 16], "float32"), "mb": ("sbuf", [128, 16], "bfloat16"),
+    "et8": ("sbuf", [128, 528], "bfloat16"), "qe8": ("sbuf", [128, 256], "float8_e4m3fn_x4"), "qe8s": ("sbuf", [128, 256], "uint8"),
+    "mask": ("sbuf", [128, C], "bfloat16"), "ik": ("sbuf", [128, KT], "int32"), "ip": ("sbuf", [128, 8], "int32"),
+    "cols": ("sbuf", [128, 16], "float32"), "plist": ("sbuf", [128, 8], "uint16"),
+    "num": ("sbuf", [128, C], "float32"), "lsr": ("sbuf", [128, 2 * C], "float32"), "yt": ("sbuf", [128, C], "float32"),
+    "rows": ("sbuf", [128, C * (3 * ROWS + 1)], "bfloat16"), "sc": ("sbuf", [128, C * SLOTS], "float16"),
+    "tf": ("sbuf", [128, KT * 3 * TABS], "float32"), "tu": ("sbuf", [128, KT * 3 * SLOTS], "uint16"),
+}
+for r in range(4):
+    SCRATCH["xt%d" % r] = ("sbuf", [128, 4 * C], "bfloat16")
+    SCRATCH["q%d" % r] = ("sbuf", [128, C], "float8_e4m3fn_x4")
+    SCRATCH["qs%d" % r] = ("sbuf", [128, C], "uint8")
+for r in range(3):
+    for k in ("f", "zt", "h", "o"):
+        SCRATCH["%s%d" % (k, r)] = ("sbuf", [128, 4 * C], "bfloat16")
+    for k in ("lq", "zq"):
+        SCRATCH["%s%d" % (k, r)] = ("sbuf", [128, C], "float8_e4m3fn_x4")
+    for k in ("lp", "zp"):
+        SCRATCH["%s%d" % (k, r)] = ("sbuf", [128, C], "uint8")
+    SCRATCH["t1l%d" % r] = ("sbuf", [128, KT], "uint16")
+    SCRATCH["t2l%d" % r] = ("sbuf", [128, 2 * KT], "uint16")
+    for k in ("sf", "sr"):
+        SCRATCH["%s%d" % (k, r)] = ("sbuf", [128, C], "float32")
+for k in ("fd", "za", "zad", "zb", "zbd"):
+    SCRATCH[k] = ("sbuf", [128, 4 * C], "bfloat16")
+for r in range(8):
+    SCRATCH["pb%d" % r] = ("psum", [128, 512], "float32")
+SEMAPHORES = ["cv", "ca", "cp", "cg", "dx0", "dx1", "du", "dl", "dw", "dv", "sent", "out"] + ["%s%d" % (k, r) for k in ("aq", "at", "au", "av") for r in range(3)]
+
+
+def rank_program(g, core, T, topo):
+    me = T.rank_of(core)
+    if me is None:
+        return
+    n_ranks = len(T.cores)
+    A, F = AluOpType, ActivationFunctionType
+    queues = {"v": g.vector, "a": g.scalar, "p": g.tensor, "g": g, "s": g.sync}
+    own = {"v": "cv", "a": "ca", "p": "cp", "g": "cg"}
+    total = {}
+    known = {q: {} for q in queues}
+    log = {}
+
+    def vw(name, a, n, step=1):
+        return (name, a, a + n * step, step)
+
+    def ap(v):
+        name, a, b, st = v
+        return T[name][:, a:b] if st == 1 else T[name][:, a:b - st + 1:st]
+
+    def wait(q, tok):
+        sem, n, clock = tok
+        if known[q].get(sem, 0) >= n:
+            return
+        queues[q].wait_ge(T.sem[sem], n)
+        known[q][sem] = n
+        for k in clock:
+            if clock[k] > known[q].get(k, 0):
+                known[q][k] = clock[k]
+
+    def order(q, kind, reads, writes):
+        deps = {}
+        for v, w in [(v, False) for v in reads] + [(v, True) for v in writes]:
+            name, a, b, st = v
+            bank = SCRATCH[name][0] == "psum"
+            for a2, b2, st2, w2, k2, tok in log.get(name, ()):
+                if k2 == kind and kind != "dma" and not (w2 and not w):
+                    continue
+                if not bank and (b2 <= a or b <= a2 or not (w or w2) or (st == st2 and st > 1 and (a - a2) % st)):
+                    continue
+                if tok[0] not in deps or deps[tok[0]][1] < tok[1]:
+                    deps[tok[0]] = tok
+        for sem in sorted(deps, key=lambda s: s == own.get(q)):
+            wait(q, deps[sem])
+
+    def note(kind, reads, writes, tok):
+        for v, w in [(v, False) for v in reads] + [(v, True) for v in writes]:
+            log.setdefault(v[0], []).append((v[1], v[2], v[3], w, kind, tok))
+
+    def do(q, make, reads, writes):
+        order(q, q, reads, writes)
+        sem = own[q]
+        total[sem] = total.get(sem, 0) + 1
+        make().then_inc(T.sem[sem], 1)
+        note(q, reads, writes, (sem, total[sem], dict(known[q])))
+
+    def dma(q, out, in_, sem, full, reads, writes):
+        order(q, "dma", reads, writes)
+        total[sem] = total.get(sem, 0) + 16
+        queues[q].dma_start(out, in_).then_inc(T.sem[sem], 16)
+        note("dma", reads, writes, (sem, full, dict(known[q])))
+
+    def ts(out, in0, s1, s2, op0, op1=None, off=None):
+        rd = [in0] + [s for s in (s1, s2) if isinstance(s, tuple)] + ([off] if off else [])
+        x1, x2 = [ap(s) if isinstance(s, tuple) else s for s in (s1, s2)]
+        src = ap(in0).indirect(ap(off)) if off else ap(in0)
+        if op1 is None:
+            do("v", lambda: g.vector.tensor_scalar(ap(out), src, x1, None, op0), rd, [out])
+        else:
+            do("v", lambda: g.vector.tensor_scalar(ap(out), src, x1, x2, op0, op1), rd, [out])
+
+    def tt(out, in0, in1, op, off=None):
+        src = ap(in0).indirect(ap(off)) if off else ap(in0)
+        do("v", lambda: g.vector.tensor_tensor(ap(out), src, ap(in1), op), [in0, in1] + ([off] if off else []), [out])
+
+    def tcopy(out, in_):
+        do("v", lambda: g.vector.tensor_copy(ap(out), ap(in_)), [in_], [out])
+
+    def act(out, in_, scale=1.0):
+        if scale == 1.0:
+            do("a", lambda: g.scalar.activation(ap(out), ap(in_), F.Copy), [in_], [out])
+        else:
+            do("a", lambda: g.scalar.activation(ap(out), ap(in_), F.Copy, scale=scale), [in_], [out])
+
+    def twin_of(b, out, in_):
+        if b % 2 == 0:
+            return act(out, in_)
+        do("g", lambda: g.affine_select(ap(out), ap(in_), [[0, C]], A.is_gt, 0.0, 1, 0), [in_], [out])
+
+    def gather(q, out, win, off):
+        if q == "v":
+            do("v", lambda: g.vector.tensor_copy(ap(out), ap(win).indirect(ap(off))), [win, off], [out])
+        else:
+            do("a", lambda: g.scalar.activation(ap(out), ap(win).indirect(ap(off)), F.Copy), [win, off], [out])
+
+    def quant(q, s, tile, a, n, at=None):
+        t = vw(tile, 4 * a if at is None else at, 4 * n)
+        do("v", lambda: g.vector.quantize_mx(ap(vw(q, a, n)), ap(vw(s, a, n)), ap(t)), [t], [vw(q, a, n), vw(s, a, n)])
+
+    def mm(bank, lq, ls, la, rq, rs, ra, n):
+        o = vw("pb%d" % bank, 0, n)
+        rd = [vw(lq, la, 128), vw(ls, la, 128), vw(rq, ra, n), vw(rs, ra, n)]
+        do("p", lambda: g.tensor.matmul_mx(ap(o), ap(rd[0]), ap(rd[1]), ap(rd[2]), ap(rd[3]), True, True), rd, [o])
+        return o
+
+    def send(dst, out, in_, sem, codes=False):
+        order("g", "g", [in_], [])
+        rid, pid = topo.addr(dst)[:2]
+        o, i = (ap(out).bitcast(dt.uint8), ap(in_).bitcast(dt.uint8)) if codes else (ap(out), ap(in_))
+        g.remote_dma(o, i, T.sem[sem], T.sem.sent, pid, rid, topo.mask(core, dst))
+        total["sent"] = total.get("sent", 0) + len(topo.engines(core, dst))
+
+    nxt = {}
+
+    def place(buf, n):
+        a = nxt.get(buf, 0)
+        nxt[buf] = a + n
+        return a
+
+    def row():
+        return place("rows", C)
+
+    def rv(a, lo=0, n=C):
+        return vw("rows", a + lo, n)
+
+    def tab():
+        return vw("tf", place("tf", KT), KT)
+
+    def off(n=KT):
+        return vw("tu", place("tu", n), n)
+
+    def part(o, lo, n):
+        return (o[0], o[1] + lo, o[1] + lo + n, 1)
+
+    mask = "mask"
+
+    def scan(out, a, lo, n):
+        o = vw("sc", out + lo, n)
+        m, x = vw(mask, lo, n), rv(a, lo, n)
+        do("v", lambda: g.vector.tensor_tensor_scan(ap(o), ap(m), ap(x), 0.0, A.add, A.max), [m, x], [o])
+
+    def picked(s):
+        return vw("sc", s + 15, KT, 16)
+
+    col = {k: vw("cols", i, 1) for i, k in enumerate(("p15", "last", "k", "turn", "half_k", "one_2k"))}
+
+    def table(a, o):
+        s = place("sc", C)
+        scan(s, a, 0, C)
+        ts(o, picked(s), col["turn"], None, A.add)
+
+    dma("s", T.xt0[:, 0:2 * C], T.x[:, 0:2 * C], "dx0", 16, [], [vw("xt0", 0, 2 * C)])
+    dma("a", T.ut[:, :], T.u[:, :], "du", 16, [], [vw("ut", 0, 512)])
+    dma("s", T.xt0[:, 2 * C:4 * C], T.x[:, 2 * C:4 * C], "dx1", 16, [], [vw("xt0", 2 * C, 2 * C)])
+    dma("a", T.lai[:, :], T.la[:, :], "dl", 32, [], [vw("lai", 0, KT)])
+    dma("a", T.lbi[:, :], T.lb[:, :], "dl", 32, [], [vw("lbi", 0, KT)])
+    wait("s", ("dx0", 16, {}))
+    wait("s", ("dx1", 16, {}))
+    dma("s", T.wq[:, :].bitcast(dt.uint8), T.wc[:, :], "dw", 32, [], [vw("wq", 0, 512)])
+    dma("s", T.wp[:, :], T.ws[:, :], "dw", 32, [], [vw("wp", 0, 512)])
+    dma("s", T.vt[:, :], T.v[:, :], "dv", 16, [], [vw("vt", 0, 512)])
+
+    do("v", lambda: g.vector.memset(T.ones[:, :], 1.0), [], [vw("ones", 0, 528)])
+    do("g", lambda: g.iota(T.im[:, :], [[1, 16]], 128, -1), [], [vw("im", 0, 16)])
+    do("g", lambda: g.iota(T.ip[:, :], [[16, 8]], 0, 0), [], [vw("ip", 0, 8)])
+    do("g", lambda: g.iota(T.ik[:, :], [[16, KT]], 0, 0), [], [vw("ik", 0, KT)])
+    do("g", lambda: g.affine_select(T.et[:, :], T.ones[:, :], [[-1, 528]], A.is_equal, 0.0, 8, 4), [vw("ones", 0, 528)], [vw("et", 0, 528)])
+    ident = row()
+    do("g", lambda: g.iota(ap(rv(ident)), [[1, C]], -int(MID), 0, allow_small_or_imprecise_dtypes=True), [], [rv(ident)])
+    do("g", lambda: g.iota(T.num[:, :], [[1, C]], 0, 0, allow_small_or_imprecise_dtypes=True), [], [vw("num", 0, C)])
+    im2 = vw("im2", 0, 16)
+    ts(im2, vw("im", 0, 16), 15, None, A.bitwise_and)
+    tcopy(vw("plist", 0, 8), vw("ip", 0, 8))
+    ts(vw("ma", 0, 16), im2, 0, -BIG, A.is_equal, A.mult)
+    ts(vw("mb", 0, 16), im2, 1, LIFT, A.is_equal, A.mult)
+    tt(vw(mask, 0, 16), vw("ma", 0, 16), vw("mb", 0, 16), A.add)
+    n = 16
+    while n < C:
+        m = min(n, C - n)
+        tcopy(vw(mask, n, m), vw(mask, 0, m))
+        n += m
+    z = tab()
+    zc = (z[0], z[1], z[1] + 1, 1)
+    ts(zc, vw("im2", 0, 1), 0, 16, A.not_equal, A.mult)
+    tt(col["p15"], zc, vw("im2", 0, 1), A.subtract)
+    ts(col["k"], vw("im2", 0, 1), 1, LIFT, A.not_equal, A.mult)
+    ts(col["turn"], col["k"], -1.0, MID, A.mult, A.add)
+    ts(col["half_k"], col["k"], 0.5, None, A.add)
+    ts(col["one_2k"], col["k"], 2.0, 1.0, A.mult, A.add)
+    num_t, low_t = tab(), tab()
+    ts(num_t, vw("ik", 0, KT), col["p15"], None, A.add)
+    ts(low_t, num_t, -MID, col["k"], A.add, A.add)
+    for b in range(4):
+        quant("qe", "qes", "et", 128 * b, 128, 8 - b)
+    quant("qu", "qus", "ut", 0, 128)
+    do("v", lambda: g.vector.tensor_copy(T.qr[:, :].bitcast(dt.uint32), T.qu[:, :].bitcast(dt.uint32).indirect(T.plist[:, 0:8])), [vw("qu", 0, 128), vw("plist", 0, 8)], [vw("qr", 0, 128)])
+    do("a", lambda: g.scalar.activation(T.qrs[:, :], T.qus[:, :].indirect(T.plist[:, 0:8]), F.Copy), [vw("qus", 0, 128), vw("plist", 0, 8)], [vw("qrs", 0, 128)])
+    act(vw("et8", 0, 528), vw("et", 0, 528), 0.125)
+    diff, base = tab(), tab()
+    lift = tab()
+
+    S_BANK = (0, 7)
+    chg_s = None
+
+    def exchange(diff, base, s):
+        sg, d2, dd, e, b2 = tab(), tab(), tab(), tab(), tab()
+        return [lambda: ts(sg, picked(s), -2.0, col["one_2k"], A.mult, A.add), lambda: tt(d2, diff, sg, A.mult), lambda: tt(dd, diff, d2, A.subtract),
+                lambda: ts(e, dd, col["half_k"], None, A.mult), lambda: tt(b2, base, e, A.add), d2, b2]
+
+    for r, d in enumerate(STEPS):
+        last = r == len(STEPS) - 1
+        dst = T.cores[(me + d) % n_ranks]
+        q, qs, xt = "q%d" % r, "qs%d" % r, "xt%d" % r
+        lq, lp, t1l, t2l = "lq%d" % r, "lp%d" % r, "t1l%d" % r, "t2l%d" % r
+        src = T.cores[(me - d) % n_ranks]
+        ne = len(topo.engines(src, core))
+        total["aq%d" % r], total["at%d" % r], total["au%d" % r] = 2 * ne, ne, ne
+        note("dma", [], [vw(lq, 0, C), vw(lp, 0, C)], ("aq%d" % r, 2 * ne, {}))
+        note("dma", [], [vw(t1l, 0, KT)], ("at%d" % r, ne, {}))
+        total["av%d" % r] = ne
+        note("dma", [], [vw(t2l, 0, KT)], ("au%d" % r, ne, {}))
+        note("dma", [], [vw(t2l, KT, KT)], ("av%d" % r, ne, {}))
+        f, zt, h, o = ["%s%d" % (k, r) for k in ("f", "zt", "h", "o")]
+        fd, za, zad, zb, zbd, hg = "fd", "za", "zad", "zb", "zbd", "zbd"
+        nxt["sc"] = 0
+
+        def plane(t, b, lo=0, n=C):
+            return vw(t, C * b + lo, n)
+
+        sv = []
+        for i in range(2):
+            quant(q, qs, xt, HALF * i, HALF)
+            sv.append(mm(S_BANK[i], "qr", "qrs", 0, q, qs, HALF * i, HALF))
+        send(dst, vw(lq, 0, C), vw(q, 0, C), "aq%d" % r, True)
+        send(dst, vw(lp, 0, C), vw(qs, 0, C), "aq%d" % r)
+        neg = row()
+        if r == 0:
+            tt(diff, vw("lbi", 0, KT), vw("lai", 0, KT), A.subtract)
+            for b in range(2):
+                quant("qe8", "qe8s", "et8", 128 * b, 128, 6 - b)
+            ts(lift, diff, col["k"], None, A.mult)
+        if chg_s is not None:
+            xs = exchange(diff, base, chg_s)
+            for n in range(3):
+                xs[n]()
+        for i in range(2):
+            ts(rv(neg, HALF * i, HALF), sv[i], 0.0, None, A.is_lt)
+            if chg_s is not None:
+                xs[3 + i]()
+            elif i == 0:
+                tt(base, vw("lai", 0, KT), lift, A.subtract)
+        if chg_s is not None:
+            diff, base = xs[5], xs[6]
+        s = place("sc", C)
+        scan(s, neg, 0, C)
+        w, p_t, to_self = tab(), tab(), tab()
+        tt(w, picked(s), diff, A.mult)
+        tt(p_t, w, base, A.add)
+        t_k = off()
+        tcopy(t_k, p_t)
+        at = row()
+        for qq, lo in (("v", 0), ("a", HALF)):
+            gather(qq, rv(at, lo, HALF), rv(ident), part(t_k, lo // 16, HALF // 16))
+        sf, sr = "sf%d" % r, "sr%d" % r
+        own_f = [mm(5 + b, "qe", "qes", 128 * b, q, qs, 0, C) for b in range(2)]
+
+        def copy_own(k):
+            b, lo = k // 2, HALF * (k % 2)
+            if k == 6:
+                act(vw(sf, 0, HALF), sv[0])
+            else:
+                act(plane(o, b, lo, HALF), part(own_f[b], lo, HALF))
+            if k in (1, 3):
+                b2 = 2 + k // 2
+                own_f.append(mm(3 + b2, "qe", "qes", 128 * b2, q, qs, 0, C))
+
+        tt(to_self, num_t, p_t, A.subtract)
+
+        low, twin = at, row()
+        tcopy(rv(twin), rv(at))
+        for k in range(7):
+            at2, low2, twin2, t2 = row(), row(), row(), off()
+            gather("a", rv(at2), rv(at), t_k)
+            copy_own(k)
+            tt(rv(low2), rv(low), rv(twin), A.min, t_k)
+            ss = place("sc", C)
+            scan(ss, at2, 0, C)
+            tcopy(rv(twin2, 0, TWIN), rv(low2, 0, TWIN))
+            ts(t2, picked(ss), col["turn"], None, A.add)
+            tcopy(rv(twin2, TWIN, C - TWIN), rv(low2, TWIN, C - TWIN))
+            at, low, twin, t_k = at2, low2, twin2, t2
+        act(vw(sf, HALF, HALF), sv[1])
+        fp = []
+        for b in range(4):
+            if b < 2:
+                fp.append(mm(1 + b, "qe", "qes", 128 * b, lq, lp, 0, C))
+                act(plane(f, b), fp[b], 0.125)
+            else:
+                fp.append(mm(1 + b, "qe8", "qe8s", 128 * (b - 2), lq, lp, 0, C))
+                act(plane(f, b), fp[b])
+        low2, twin2, m = row(), row(), row()
+        tt(rv(low2), rv(low), rv(twin), A.min, t_k)
+        tcopy(rv(twin2, 0, 128), rv(low2, 0, 128))
+        s = place("sc", C)
+        o1, x1 = vw("sc", s + 128, C - 128), rv(low2, 128, C - 128)
+        mk = vw(mask, 128, C - 128)
+        do("v", lambda: g.vector.tensor_tensor_scan(ap(o1), ap(mk), ap(x1), 0.0, A.add, A.max), [mk, x1], [o1])
+        tt(rv(m, 0, 128), rv(low2), rv(twin2, 0, 128), A.min, part(t_k, 0, 8))
+        scan(s, m, 0, 128)
+        eq, mv, t_f, tears = tab(), tab(), tab(), off()
+        tt(eq, picked(s), low_t, A.is_equal)
+        tt(mv, eq, to_self, A.mult)
+        tt(t_f, mv, p_t, A.add)
+        tcopy(tears, t_f)
+        send(dst, vw(t1l, 0, KT), tears, "at%d" % r)
+
+        tr, tr2, tr4 = row(), row(), row()
+        both = off(2 * KT)
+        jump2, jump4 = part(both, 0, KT), part(both, KT, KT)
+        for out, win in ((tr, ident), (tr2, tr)):
+            for qq, lo in (("v", 0), ("a", HALF)):
+                gather(qq, rv(out, lo, HALF), rv(win), part(tears, lo // 16, HALF // 16))
+        act(plane(fd, 0), plane(f, 0))
+        table(tr2, jump2)
+        send(dst, vw(t2l, 0, KT), jump2, "au%d" % r)
+        gather("a", rv(tr4), rv(tr2), jump2)
+        tcopy(rv(twin2, 128, C - 128), rv(low2, 128, C - 128))
+        tt(rv(m, 128, C - 128), rv(low2), rv(twin2, 128, C - 128), A.min, part(t_k, 8, KT - 8))
+        table(tr4, jump4)
+        send(dst, vw(t2l, KT, KT), jump4, "av%d" % r)
+        if r == 0:
+            quant("qv", "qvs", "vt", 0, 128)
+        act(plane(fd, 1), plane(f, 1))
+
+        lead = [m, row(), row(), row()]
+        for b in range(2, 4):
+            gather("a", plane(fd, b), plane(f, b), vw(t1l, 0, KT))
+        for b in range(4):
+            if b < 2:
+                tt(plane(za, b), plane(f, b), plane(fd, b), A.add, vw(t1l, 0, KT))
+            else:
+                tt(plane(za, b), fp[b], plane(fd, b), A.add)
+            twin_of(b, plane(zad, b), plane(za, b))
+        gather("a", rv(lead[1]), rv(m), t_k)
+        act(plane(o, 3, 0, HALF), part(own_f[3], 0, HALF))
+        for b in range(4):
+            tt(plane(zb, b), plane(za, b), plane(zad, b), A.add, vw(t2l, 0, KT))
+            if b == 1:
+                gather("a", rv(lead[2]), rv(lead[1]), t_k)
+            twin_of(b, plane(zbd, b), plane(zb, b))
+        gather("a", rv(lead[3]), rv(lead[2]), t_k)
+        for b in range(4):
+            tt(vw(zt, b, C, 4), plane(zb, b), plane(zbd, b), A.add, vw(t2l, KT, KT))
+            if b == 2:
+                t_r = off()
+                table(lead[3], t_r)
+                for i in range(2):
+                    gather("a", vw(sr, HALF * i, HALF), vw(sf, 0, C), part(t_r, HALF * i // 16, HALF // 16))
+        zq, zp = "zq%d" % r, "zp%d" % r
+        for i in range(2):
+            quant(zq, zp, zt, HALF * i, HALF)
+            hb = mm((1, 5)[i], "wq", "wp", 0, zq, zp, HALF * i, HALF)
+            act(plane(h, 0, HALF * i, HALF), hb, 0.03125)
+        for b in range(1, 4):
+            hb = mm(1 + b, "wq", "wp", 128 * b, zq, zp, 0, C)
+            act(plane(h, b), hb, 0.03125)
+        chg = row()
+        for i in range(2):
+            tt(rv(chg, HALF * i, HALF), sv[i], vw(sr, HALF * i, HALF), A.is_lt)
+        chg_s = place("sc", C)
+        scan(chg_s, chg, 0, C)
+
+        x2 = "xt%d" % (r + 1)
+        if not last:
+            gather("a", plane(hg, 3, HALF, HALF), plane(h, 3), part(tears, KT // 2, KT // 2))
+            for b in range(3):
+                tt(vw(x2, b, C, 4), plane(h, b), plane(o, b), A.add, tears)
+            tt(vw(x2, 3, HALF, 4), plane(h, 3), plane(o, 3, 0, HALF), A.add, part(tears, 0, KT // 2))
+            tt(vw(x2, 4 * HALF + 3, HALF, 4), part(own_f[3], HALF, HALF), plane(hg, 3, HALF, HALF), A.add)
+    q, qs = "q3", "qs3"
+    for i in range(2):
+        lo = HALF * i
+        if i == 0:
+            gather("a", plane(hg, 3, HALF, HALF), plane(h, 3), part(tears, KT // 2, KT // 2))
+            xs = exchange(diff, base, chg_s)
+            d2, b2 = xs[5], xs[6]
+            lift, l0, l1, t0, t1 = tab(), tab(), tab(), off(), off()
+            steps = xs[:5] + [lambda: ts(lift, d2, col["k"], None, A.mult), lambda: tt(l0, lift, b2, A.add), lambda: tcopy(t0, l0),
+                              lambda: tt(l1, l0, d2, A.add), lambda: tcopy(t1, l1)]
+        for b in range(4 - i):
+            tt(vw(x2, 4 * lo + b, HALF, 4), plane(h, b), plane(o, b, lo, HALF), A.add, part(tears, lo // 16, HALF // 16))
+            steps.pop(0)()
+        if i == 1:
+            for n, t in enumerate((t0, t1)):
+                gather("a", vw("lsr", C * n, C), vw("num", 0, C), t)
+            tt(vw(x2, 4 * lo + 3, HALF, 4), part(own_f[3], lo, HALF), plane(hg, 3, lo, HALF), A.add)
+        quant(q, qs, x2, lo, HALF)
+        yb = mm((0, 7)[i], "qv", "qvs", 0, q, qs, lo, HALF)
+        qv = vw(q, lo, HALF)
+        dma("s", T.oc[:, 4 * lo:4 * lo + 4 * HALF], ap(qv).bitcast(dt.uint8), "out", 0, [qv], [])
+        for k in range(4):
+            dma("s", T.osc[4 * k:4 * k + 4, lo:lo + HALF], T[qs][32 * k:32 * k + 4, lo:lo + HALF], "out", 0, [vw(qs, lo, HALF)], [])
+        yv = vw("yt", lo, HALF)
+        if i == 0:
+            act(yv, yb)
+            for n in range(3):
+                steps.pop(0)()
+        else:
+            ts(yv, yb, 1.0, None, A.mult)
+        dma("as"[i], T.y[:, lo:lo + HALF], ap(yv), "out", 0, [yv], [])
+    dma("a", T.ls[:, :], T.lsr[0:128:16, :], "out", 0, [vw("lsr", 0, 2 * C)], [])
+    for sem in sorted(total):
+        if known["g"].get(sem, 0) < total[sem]:
+            g.wait_ge(T.sem[sem], total[sem])

@@ -5,11 +5,14 @@ C = 384
 HALF = C // 2
 STEPS = [1, 2, 3]
 KT = C // 16
-TWIN = 128
+KH = KT // 2
+CUT = 192
 ROWS = 34
 SLOTS = 14
 TABS = 20
 BIG, LIFT, MID = 2048.0, 512.0, 192.0
+TINY = 2.0 ** -100
+OPT = {}
 
 SCRATCH = {
     "ut": ("sbuf", [128, 512], "bfloat16"), "qu": ("sbuf", [128, 128], "float8_e4m3fn_x4"), "qus": ("sbuf", [128, 128], "uint8"),
@@ -19,13 +22,14 @@ SCRATCH = {
     "ones": ("sbuf", [128, 528], "bfloat16"), "et": ("sbuf", [128, 528], "bfloat16"),
     "qe": ("sbuf", [128, 512], "float8_e4m3fn_x4"), "qes": ("sbuf", [128, 512], "uint8"),
     "lai": ("sbuf", [128, KT], "int32"), "lbi": ("sbuf", [128, KT], "int32"),
-    "im": ("sbuf", [128, 16], "int32"), "im2": ("sbuf", [128, 16], "int32"), "ma": ("sbuf", [128, 16], "float32"), "mb": ("sbuf", [128, 16], "bfloat16"),
+    "im": ("sbuf", [128, 48], "int32"), "im2": ("sbuf", [128, 48], "int32"), "ma": ("sbuf", [128, 48], "bfloat16"), "mb": ("sbuf", [128, 48], "bfloat16"),
     "et8": ("sbuf", [128, 528], "bfloat16"), "qe8": ("sbuf", [128, 256], "float8_e4m3fn_x4"), "qe8s": ("sbuf", [128, 256], "uint8"),
     "mask": ("sbuf", [128, C], "bfloat16"), "ik": ("sbuf", [128, KT], "int32"), "ip": ("sbuf", [128, 8], "int32"),
     "cols": ("sbuf", [128, 16], "float32"), "plist": ("sbuf", [128, 8], "uint16"),
     "num": ("sbuf", [128, C], "float32"), "lsr": ("sbuf", [128, 2 * C], "float32"), "yt": ("sbuf", [128, C], "float32"),
     "rows": ("sbuf", [128, C * (3 * ROWS + 1)], "bfloat16"), "sc": ("sbuf", [128, C * SLOTS], "float16"),
     "tf": ("sbuf", [128, KT * 3 * TABS], "float32"), "tu": ("sbuf", [128, KT * 3 * SLOTS], "uint16"),
+    "te": ("sbuf", [128, 2 * KT], "float32"),
 }
 for r in range(4):
     SCRATCH["xt%d" % r] = ("sbuf", [128, 4 * C], "bfloat16")
@@ -110,14 +114,13 @@ def rank_program(g, core, T, topo):
         queues[q].dma_start(out, in_).then_inc(T.sem[sem], 16)
         note("dma", reads, writes, (sem, full, dict(known[q])))
 
-    def ts(out, in0, s1, s2, op0, op1=None, off=None):
-        rd = [in0] + [s for s in (s1, s2) if isinstance(s, tuple)] + ([off] if off else [])
+    def ts(out, in0, s1, s2, op0, op1=None):
+        rd = [in0] + [s for s in (s1, s2) if isinstance(s, tuple)]
         x1, x2 = [ap(s) if isinstance(s, tuple) else s for s in (s1, s2)]
-        src = ap(in0).indirect(ap(off)) if off else ap(in0)
         if op1 is None:
-            do("v", lambda: g.vector.tensor_scalar(ap(out), src, x1, None, op0), rd, [out])
+            do("v", lambda: g.vector.tensor_scalar(ap(out), ap(in0), x1, None, op0), rd, [out])
         else:
-            do("v", lambda: g.vector.tensor_scalar(ap(out), src, x1, x2, op0, op1), rd, [out])
+            do("v", lambda: g.vector.tensor_scalar(ap(out), ap(in0), x1, x2, op0, op1), rd, [out])
 
     def tt(out, in0, in1, op, off=None):
         src = ap(in0).indirect(ap(off)) if off else ap(in0)
@@ -132,10 +135,12 @@ def rank_program(g, core, T, topo):
         else:
             do("a", lambda: g.scalar.activation(ap(out), ap(in_), F.Copy, scale=scale), [in_], [out])
 
-    def twin_of(b, out, in_):
-        if b % 2 == 0:
+    def copy_on(q, out, in_):
+        if q == "a":
             return act(out, in_)
-        do("g", lambda: g.affine_select(ap(out), ap(in_), [[0, C]], A.is_gt, 0.0, 1, 0), [in_], [out])
+        if q == "v":
+            return tcopy(out, in_)
+        do("g", lambda: g.affine_select(ap(out), ap(in_), [[0, out[2] - out[1]]], A.is_gt, 0.0, 1, 0), [in_], [out])
 
     def gather(q, out, win, off):
         if q == "v":
@@ -182,22 +187,24 @@ def rank_program(g, core, T, topo):
     def part(o, lo, n):
         return (o[0], o[1] + lo, o[1] + lo + n, 1)
 
+    def cols_of(t, lo, n):
+        return part(t, lo // 16, n // 16)
+
     mask = "mask"
 
+    def scan_of(o, d0, d1, op0, op1):
+        do("v", lambda: g.vector.tensor_tensor_scan(ap(o), ap(d0), ap(d1), 0.0, op0, op1), [d0, d1], [o])
+
     def scan(out, a, lo, n):
-        o = vw("sc", out + lo, n)
-        m, x = vw(mask, lo, n), rv(a, lo, n)
-        do("v", lambda: g.vector.tensor_tensor_scan(ap(o), ap(m), ap(x), 0.0, A.add, A.max), [m, x], [o])
+        scan_of(vw("sc", out + lo, n), vw(mask, lo, n), rv(a, lo, n), A.add, A.max)
 
-    def picked(s):
-        return vw("sc", s + 15, KT, 16)
+    def picked(s, lo=0, n=C):
+        return vw("sc", s + lo + 15, n // 16, 16)
 
-    col = {k: vw("cols", i, 1) for i, k in enumerate(("p15", "last", "k", "turn", "half_k", "one_2k"))}
+    col = {k: vw("cols", i, 1) for i, k in enumerate(("p15", "z", "k", "turn", "one_2k"))}
 
-    def table(a, o):
-        s = place("sc", C)
-        scan(s, a, 0, C)
-        ts(o, picked(s), col["turn"], None, A.add)
+    def turn(o, s, lo=0, n=C):
+        ts(cols_of(o, lo, n), picked(s, lo, n), col["turn"], None, A.add)
 
     dma("s", T.xt0[:, 0:2 * C], T.x[:, 0:2 * C], "dx0", 16, [], [vw("xt0", 0, 2 * C)])
     dma("a", T.ut[:, :], T.u[:, :], "du", 16, [], [vw("ut", 0, 512)])
@@ -210,52 +217,53 @@ def rank_program(g, core, T, topo):
     dma("s", T.wp[:, :], T.ws[:, :], "dw", 32, [], [vw("wp", 0, 512)])
     dma("s", T.vt[:, :], T.v[:, :], "dv", 16, [], [vw("vt", 0, 512)])
 
+    W = 48
+    do("g", lambda: g.iota(T.im[:, :], [[1, W]], 128, -1), [], [vw("im", 0, W)])
     do("v", lambda: g.vector.memset(T.ones[:, :], 1.0), [], [vw("ones", 0, 528)])
-    do("g", lambda: g.iota(T.im[:, :], [[1, 16]], 128, -1), [], [vw("im", 0, 16)])
+    do("g", lambda: g.affine_select(T.et[:, :], T.ones[:, :], [[-1, 528]], A.is_equal, 0.0, 8, 4), [vw("ones", 0, 528)], [vw("et", 0, 528)])
     do("g", lambda: g.iota(T.ip[:, :], [[16, 8]], 0, 0), [], [vw("ip", 0, 8)])
     do("g", lambda: g.iota(T.ik[:, :], [[16, KT]], 0, 0), [], [vw("ik", 0, KT)])
-    do("g", lambda: g.affine_select(T.et[:, :], T.ones[:, :], [[-1, 528]], A.is_equal, 0.0, 8, 4), [vw("ones", 0, 528)], [vw("et", 0, 528)])
     ident = row()
     do("g", lambda: g.iota(ap(rv(ident)), [[1, C]], -int(MID), 0, allow_small_or_imprecise_dtypes=True), [], [rv(ident)])
-    do("g", lambda: g.iota(T.num[:, :], [[1, C]], 0, 0, allow_small_or_imprecise_dtypes=True), [], [vw("num", 0, C)])
-    im2 = vw("im2", 0, 16)
-    ts(im2, vw("im", 0, 16), 15, None, A.bitwise_and)
-    tcopy(vw("plist", 0, 8), vw("ip", 0, 8))
-    ts(vw("ma", 0, 16), im2, 0, -BIG, A.is_equal, A.mult)
-    ts(vw("mb", 0, 16), im2, 1, LIFT, A.is_equal, A.mult)
-    tt(vw(mask, 0, 16), vw("ma", 0, 16), vw("mb", 0, 16), A.add)
-    n = 16
-    while n < C:
-        m = min(n, C - n)
-        tcopy(vw(mask, n, m), vw(mask, 0, m))
-        n += m
-    z = tab()
-    zc = (z[0], z[1], z[1] + 1, 1)
-    ts(zc, vw("im2", 0, 1), 0, 16, A.not_equal, A.mult)
-    tt(col["p15"], zc, vw("im2", 0, 1), A.subtract)
-    ts(col["k"], vw("im2", 0, 1), 1, LIFT, A.not_equal, A.mult)
+    im2 = vw("im2", 0, W)
+    first = vw("im2", 0, 1)
+    ts(im2, vw("im", 0, W), 15, None, A.bitwise_and)
+    do("v", lambda: g.vector.memset(T.te[:, :], 0.0), [], [vw("te", 0, 2 * KT)])
+    ts(vw("ma", 0, W), im2, 0, -BIG, A.is_equal, A.mult)
+    ts(vw("mb", 0, W), im2, 1, LIFT, A.is_equal, A.mult)
+    ts(col["z"], first, 0, 16, A.not_equal, A.mult)
+    ts(col["k"], first, 1, LIFT, A.not_equal, A.mult)
+    tt(vw(mask, 0, W), vw("ma", 0, W), vw("mb", 0, W), A.add)
+    tt(col["p15"], col["z"], first, A.subtract)
+    tcopy(vw(mask, W, W), vw(mask, 0, W))
     ts(col["turn"], col["k"], -1.0, MID, A.mult, A.add)
-    ts(col["half_k"], col["k"], 0.5, None, A.add)
+    tcopy(vw(mask, 2 * W, 2 * W), vw(mask, 0, 2 * W))
     ts(col["one_2k"], col["k"], 2.0, 1.0, A.mult, A.add)
-    num_t, low_t = tab(), tab()
-    ts(num_t, vw("ik", 0, KT), col["p15"], None, A.add)
-    ts(low_t, num_t, -MID, col["k"], A.add, A.add)
+    tcopy(vw(mask, 4 * W, 4 * W), vw(mask, 0, 4 * W))
+    act(vw("et8", 0, 528), vw("et", 0, 528), 0.125)
+    num_t, low_t, k_t = tab(), tab(), tab()
     for b in range(4):
         quant("qe", "qes", "et", 128 * b, 128, 8 - b)
+    tcopy(vw("plist", 0, 8), vw("ip", 0, 8))
     quant("qu", "qus", "ut", 0, 128)
+    ts(num_t, vw("ik", 0, KT), col["p15"], None, A.add)
     do("v", lambda: g.vector.tensor_copy(T.qr[:, :].bitcast(dt.uint32), T.qu[:, :].bitcast(dt.uint32).indirect(T.plist[:, 0:8])), [vw("qu", 0, 128), vw("plist", 0, 8)], [vw("qr", 0, 128)])
     do("a", lambda: g.scalar.activation(T.qrs[:, :], T.qus[:, :].indirect(T.plist[:, 0:8]), F.Copy), [vw("qus", 0, 128), vw("plist", 0, 8)], [vw("qrs", 0, 128)])
-    act(vw("et8", 0, 528), vw("et", 0, 528), 0.125)
-    diff, base = tab(), tab()
-    lift = tab()
+    ts(low_t, num_t, -MID, col["k"], A.add, A.add)
+    ts(k_t, vw("ik", 0, KT), HALF, col["k"], A.is_ge, A.add)
+    for b in range(2):
+        quant("qe8", "qe8s", "et8", 128 * b, 128, 6 - b)
+    whole, mid, half, k_half, base = tab(), tab(), tab(), tab(), tab()
+    steps = [lambda: tt(whole, vw("lai", 0, KT), vw("lbi", 0, KT), A.subtract), lambda: ts(half, whole, 0.5, None, A.mult),
+             lambda: tt(mid, half, vw("lbi", 0, KT), A.add), lambda: tt(k_half, half, k_t, A.mult), lambda: tt(base, mid, k_half, A.subtract)]
 
     S_BANK = (0, 7)
-    chg_s = None
+    HALVES = ((0, HALF), (HALF, HALF))
+    CUTS = ((0, CUT), (CUT, C - CUT))
 
-    def exchange(diff, base, s):
-        sg, d2, dd, e, b2 = tab(), tab(), tab(), tab(), tab()
-        return [lambda: ts(sg, picked(s), -2.0, col["one_2k"], A.mult, A.add), lambda: tt(d2, diff, sg, A.mult), lambda: tt(dd, diff, d2, A.subtract),
-                lambda: ts(e, dd, col["half_k"], None, A.mult), lambda: tt(b2, base, e, A.add), d2, b2]
+    def run(steps, n):
+        for _ in range(min(n, len(steps))):
+            steps.pop(0)()
 
     for r, d in enumerate(STEPS):
         last = r == len(STEPS) - 1
@@ -264,14 +272,14 @@ def rank_program(g, core, T, topo):
         lq, lp, t1l, t2l = "lq%d" % r, "lp%d" % r, "t1l%d" % r, "t2l%d" % r
         src = T.cores[(me - d) % n_ranks]
         ne = len(topo.engines(src, core))
-        total["aq%d" % r], total["at%d" % r], total["au%d" % r] = 2 * ne, ne, ne
+        total["aq%d" % r], total["at%d" % r], total["au%d" % r], total["av%d" % r] = 2 * ne, ne, ne, ne
         note("dma", [], [vw(lq, 0, C), vw(lp, 0, C)], ("aq%d" % r, 2 * ne, {}))
-        note("dma", [], [vw(t1l, 0, KT)], ("at%d" % r, ne, {}))
-        total["av%d" % r] = ne
-        note("dma", [], [vw(t2l, 0, KT)], ("au%d" % r, ne, {}))
-        note("dma", [], [vw(t2l, KT, KT)], ("av%d" % r, ne, {}))
+        got1, got2, got4 = vw(t1l, 0, KT), vw(t2l, 0, KT), vw(t2l, KT, KT)
+        for t, sem in ((got1, "at"), (got2, "au"), (got4, "av")):
+            note("dma", [], [t], ("%s%d" % (sem, r), ne, {}))
         f, zt, h, o = ["%s%d" % (k, r) for k in ("f", "zt", "h", "o")]
         fd, za, zad, zb, zbd, hg = "fd", "za", "zad", "zb", "zbd", "zbd"
+        sf, sr = "sf%d" % r, "sr%d" % r
         nxt["sc"] = 0
 
         def plane(t, b, lo=0, n=C):
@@ -281,132 +289,162 @@ def rank_program(g, core, T, topo):
         for i in range(2):
             quant(q, qs, xt, HALF * i, HALF)
             sv.append(mm(S_BANK[i], "qr", "qrs", 0, q, qs, HALF * i, HALF))
+            if r == 0:
+                run(steps, 1)
         send(dst, vw(lq, 0, C), vw(q, 0, C), "aq%d" % r, True)
         send(dst, vw(lp, 0, C), vw(qs, 0, C), "aq%d" % r)
-        neg = row()
         if r == 0:
-            tt(diff, vw("lbi", 0, KT), vw("lai", 0, KT), A.subtract)
-            for b in range(2):
-                quant("qe8", "qe8s", "et8", 128 * b, 128, 6 - b)
-            ts(lift, diff, col["k"], None, A.mult)
-        if chg_s is not None:
-            xs = exchange(diff, base, chg_s)
-            for n in range(3):
-                xs[n]()
-        for i in range(2):
-            ts(rv(neg, HALF * i, HALF), sv[i], 0.0, None, A.is_lt)
-            if chg_s is not None:
-                xs[3 + i]()
-            elif i == 0:
-                tt(base, vw("lai", 0, KT), lift, A.subtract)
-        if chg_s is not None:
-            diff, base = xs[5], xs[6]
+            do("g", lambda: g.iota(T.num[:, :], [[1, C]], 0, 0, allow_small_or_imprecise_dtypes=True), [], [vw("num", 0, C)])
+        own_f = [mm(5 + b, "qe", "qes", 128 * b, q, qs, 0, C) for b in range(2)]
+        side = row()
+        do("a", lambda: g.scalar.activation(ap(rv(side, 0, HALF)), ap(sv[0]), F.Sign, bias=TINY), [sv[0]], [rv(side, 0, HALF)])
+        act(vw(sf, 0, HALF), sv[0])
+        run(steps, len(steps) - 1)
+        ts(rv(side, HALF, HALF), sv[1], 0.0, 2.0, A.is_ge, A.mult)
+        act(vw(sf, HALF, HALF), sv[1])
+        run(steps, 1)
         s = place("sc", C)
-        scan(s, neg, 0, C)
-        w, p_t, to_self = tab(), tab(), tab()
-        tt(w, picked(s), diff, A.mult)
+        scan(s, side, 0, C)
+        w, pair = tab(), place("tf", 2 * KT)
+        to_self, p_t = vw("tf", pair, KT, 2), vw("tf", pair + 1, KT, 2)
+        tt(w, picked(s), half, A.mult)
         tt(p_t, w, base, A.add)
         t_k = off()
         tcopy(t_k, p_t)
-        at = row()
-        for qq, lo in (("v", 0), ("a", HALF)):
-            gather(qq, rv(at, lo, HALF), rv(ident), part(t_k, lo // 16, HALF // 16))
-        sf, sr = "sf%d" % r, "sr%d" % r
-        own_f = [mm(5 + b, "qe", "qes", 128 * b, q, qs, 0, C) for b in range(2)]
 
-        def copy_own(k):
+        def unpack_own(k):
             b, lo = k // 2, HALF * (k % 2)
-            if k == 6:
-                act(vw(sf, 0, HALF), sv[0])
-            else:
-                act(plane(o, b, lo, HALF), part(own_f[b], lo, HALF))
+            act(plane(o, b, lo, HALF), part(own_f[b], lo, HALF))
             if k in (1, 3):
                 b2 = 2 + k // 2
                 own_f.append(mm(3 + b2, "qe", "qes", 128 * b2, q, qs, 0, C))
 
-        tt(to_self, num_t, p_t, A.subtract)
+        fp = []
+
+        def unpack_src(b, out, lo, n):
+            if len(fp) == b:
+                e, es, ea = ("qe", "qes", 128 * b) if b < 2 else ("qe8", "qe8s", 128 * (b - 2))
+                fp.append(mm(1 + b, e, es, ea, lq, lp, 0, C))
+            act(plane(out, b, lo, n), part(fp[b], lo, n), 0.125 if b < 2 else 1.0)
+
+        spare = [lambda k=k: unpack_own(k) for k in range(7)] + [lambda lo=lo: unpack_src(0, f, lo, HALF) for lo in (0, HALF)]
+        run(spare, OPT.get("early", 2))
+        at = row()
+        for qq, (lo, n) in zip("va", HALVES):
+            gather(qq, rv(at, lo, n), rv(ident), cols_of(t_k, lo, n))
 
         low, twin = at, row()
         tcopy(rv(twin), rv(at))
+        behind = None
         for k in range(7):
             at2, low2, twin2, t2 = row(), row(), row(), off()
-            gather("a", rv(at2), rv(at), t_k)
-            copy_own(k)
-            tt(rv(low2), rv(low), rv(twin), A.min, t_k)
             ss = place("sc", C)
-            scan(ss, at2, 0, C)
-            tcopy(rv(twin2, 0, TWIN), rv(low2, 0, TWIN))
-            ts(t2, picked(ss), col["turn"], None, A.add)
-            tcopy(rv(twin2, TWIN, C - TWIN), rv(low2, TWIN, C - TWIN))
+            for i in range(2):
+                (lo, n), (lo2, n2) = HALVES[i], CUTS[i]
+                gather("a", rv(at2, lo, n), rv(at), cols_of(t_k, lo, n))
+                if i == 0 and behind:
+                    behind()
+                if i == 1:
+                    run(spare, 1)
+                if k == 0 and i == 0:
+                    tt(rv(low2, lo2, n2), rv(low), rv(twin, lo2, n2), A.min, cols_of(t_k, lo2, n2))
+                    scan(ss, at2, lo, n)
+                    tt(to_self, num_t, p_t, A.subtract)
+                else:
+                    scan(ss, at2, lo, n)
+                    tt(rv(low2, lo2, n2), rv(low), rv(twin, lo2, n2), A.min, cols_of(t_k, lo2, n2))
+                if i == 0:
+                    copy_on(OPT.get("tw", "g"), rv(twin2, lo2, n2), rv(low2, lo2, n2))
+                else:
+                    behind = lambda a=twin2, b=low2, lo=lo2, n=n2: copy_on("a", rv(a, lo, n), rv(b, lo, n))
+                turn(t2, ss, lo, n)
             at, low, twin, t_k = at2, low2, twin2, t2
-        act(vw(sf, HALF, HALF), sv[1])
-        fp = []
-        for b in range(4):
-            if b < 2:
-                fp.append(mm(1 + b, "qe", "qes", 128 * b, lq, lp, 0, C))
-                act(plane(f, b), fp[b], 0.125)
-            else:
-                fp.append(mm(1 + b, "qe8", "qe8s", 128 * (b - 2), lq, lp, 0, C))
-                act(plane(f, b), fp[b])
-        low2, twin2, m = row(), row(), row()
-        tt(rv(low2), rv(low), rv(twin), A.min, t_k)
-        tcopy(rv(twin2, 0, 128), rv(low2, 0, 128))
+        behind()
+        run(spare, 9)
+        far, m = row(), row()
+        for lo, n in CUTS:
+            tt(rv(far, lo, n), rv(low), rv(twin, lo, n), A.min, cols_of(t_k, lo, n))
+        unpack_src(1, f, 0, C)
+        copy_on("g", plane(fd, 0), plane(f, 0))
+        for b in range(2, 4):
+            unpack_src(b, f, 0, C)
+        unpack_src(1, fd, 0, C)
         s = place("sc", C)
-        o1, x1 = vw("sc", s + 128, C - 128), rv(low2, 128, C - 128)
-        mk = vw(mask, 128, C - 128)
-        do("v", lambda: g.vector.tensor_tensor_scan(ap(o1), ap(mk), ap(x1), 0.0, A.add, A.max), [mk, x1], [o1])
-        tt(rv(m, 0, 128), rv(low2), rv(twin2, 0, 128), A.min, part(t_k, 0, 8))
+        tt(rv(m, 0, 128), rv(far), rv(low, 0, 128), A.min, cols_of(t_k, 0, 128))
+        scan(s, far, 128, C - 128)
         scan(s, m, 0, 128)
-        eq, mv, t_f, tears = tab(), tab(), tab(), off()
-        tt(eq, picked(s), low_t, A.is_equal)
-        tt(mv, eq, to_self, A.mult)
-        tt(t_f, mv, p_t, A.add)
-        tcopy(tears, t_f)
-        send(dst, vw(t1l, 0, KT), tears, "at%d" % r)
+        both, tears = place("tf", 2 * KT), off()
+        tt(vw("te", 1, KT, 2), picked(s), low_t, A.is_equal)
+        scan_of(vw("tf", both, 2 * KT), vw("te", 0, 2 * KT), vw("tf", pair, 2 * KT), A.mult, A.add)
+        tcopy(tears, vw("tf", both + 1, KT, 2))
+        send(dst, got1, tears, "at%d" % r)
 
         tr, tr2, tr4 = row(), row(), row()
-        both = off(2 * KT)
-        jump2, jump4 = part(both, 0, KT), part(both, KT, KT)
-        for out, win in ((tr, ident), (tr2, tr)):
-            for qq, lo in (("v", 0), ("a", HALF)):
-                gather(qq, rv(out, lo, HALF), rv(win), part(tears, lo // 16, HALF // 16))
-        act(plane(fd, 0), plane(f, 0))
-        table(tr2, jump2)
-        send(dst, vw(t2l, 0, KT), jump2, "au%d" % r)
-        gather("a", rv(tr4), rv(tr2), jump2)
-        tcopy(rv(twin2, 128, C - 128), rv(low2, 128, C - 128))
-        tt(rv(m, 128, C - 128), rv(low2), rv(twin2, 128, C - 128), A.min, part(t_k, 8, KT - 8))
-        table(tr4, jump4)
-        send(dst, vw(t2l, KT, KT), jump4, "av%d" % r)
+        jump2, jump4 = off(), off()
+        for j, (out, win) in enumerate(((tr, ident), (tr2, tr))):
+            for qq, (lo, n) in zip("va", HALVES):
+                gather(qq, rv(out, lo, n), rv(win), cols_of(tears, lo, n))
+            lo = 128 * (j + 1)
+            tt(rv(m, lo, 128), rv(far), rv(low, lo, 128), A.min, cols_of(t_k, lo, 128))
+        s = place("sc", C)
+        scan(s, tr2, 0, C)
         if r == 0:
             quant("qv", "qvs", "vt", 0, 128)
-        act(plane(fd, 1), plane(f, 1))
+        turn(jump2, s)
+        send(dst, got2, jump2, "au%d" % r)
 
         lead = [m, row(), row(), row()]
-        for b in range(2, 4):
-            gather("a", plane(fd, b), plane(f, b), vw(t1l, 0, KT))
-        for b in range(4):
+
+        def z1(b):
             if b < 2:
-                tt(plane(za, b), plane(f, b), plane(fd, b), A.add, vw(t1l, 0, KT))
+                tt(plane(za, b), plane(f, b), plane(fd, b), A.add, got1)
             else:
                 tt(plane(za, b), fp[b], plane(fd, b), A.add)
-            twin_of(b, plane(zad, b), plane(za, b))
-        gather("a", rv(lead[1]), rv(m), t_k)
-        act(plane(o, 3, 0, HALF), part(own_f[3], 0, HALF))
-        for b in range(4):
-            tt(plane(zb, b), plane(za, b), plane(zad, b), A.add, vw(t2l, 0, KT))
+
+        def z2(b):
+            tt(plane(zb, b), plane(za, b), plane(zad, b), A.add, got2)
+
+        def z3(b):
+            tt(vw(zt, b, C, 4), plane(zb, b), plane(zbd, b), A.add, got4)
+
+        def follow(j):
+            gather("a", rv(lead[j + 1]), rv(lead[j]), t_k)
+
+        if OPT.get("lead1", 1):
+            follow(0)
+        gather("a", plane(fd, 2), plane(f, 2), got1)
+        gather("a", rv(tr4), rv(tr2), jump2)
+        gather("a", plane(fd, 3), plane(f, 3), got1)
+        for b in range(3):
+            z1(b)
+            copy_on("gga"[b], plane(zad, b), plane(za, b))
+        s = place("sc", C)
+        scan(s, tr4, 0, C)
+        z2(0)
+        turn(jump4, s)
+        send(dst, got4, jump4, "av%d" % r)
+        z1(3)
+        copy_on("a", plane(zad, 3), plane(za, 3))
+        copy_on("g", plane(zbd, 0), plane(zb, 0))
+        if not OPT.get("lead1", 1):
+            follow(0)
+        follow(1)
+        for b in range(1, 4):
+            z2(b)
+            copy_on("aga"[b - 1], plane(zbd, b), plane(zb, b))
             if b == 1:
-                gather("a", rv(lead[2]), rv(lead[1]), t_k)
-            twin_of(b, plane(zbd, b), plane(zb, b))
-        gather("a", rv(lead[3]), rv(lead[2]), t_k)
-        for b in range(4):
-            tt(vw(zt, b, C, 4), plane(zb, b), plane(zbd, b), A.add, vw(t2l, KT, KT))
-            if b == 2:
-                t_r = off()
-                table(lead[3], t_r)
-                for i in range(2):
-                    gather("a", vw(sr, HALF * i, HALF), vw(sf, 0, C), part(t_r, HALF * i // 16, HALF // 16))
+                follow(2)
+        z3(0)
+        s, t_r = place("sc", C), off()
+        scan(s, lead[3], 0, C)
+        z3(1)
+        turn(t_r, s)
+        for lo, n in HALVES:
+            gather("a", vw(sr, lo, n), vw(sf, 0, C), cols_of(t_r, lo, n))
+        z3(2)
+        z3(3)
         zq, zp = "zq%d" % r, "zp%d" % r
+        chg = row()
         for i in range(2):
             quant(zq, zp, zt, HALF * i, HALF)
             hb = mm((1, 5)[i], "wq", "wp", 0, zq, zp, HALF * i, HALF)
@@ -414,35 +452,36 @@ def rank_program(g, core, T, topo):
         for b in range(1, 4):
             hb = mm(1 + b, "wq", "wp", 128 * b, zq, zp, 0, C)
             act(plane(h, b), hb, 0.03125)
-        chg = row()
-        for i in range(2):
-            tt(rv(chg, HALF * i, HALF), sv[i], vw(sr, HALF * i, HALF), A.is_lt)
         chg_s = place("sc", C)
-        scan(chg_s, chg, 0, C)
+        for i, (lo, n) in enumerate(HALVES):
+            tt(rv(chg, lo, n), sv[i], vw(sr, lo, n), A.is_lt)
+        for lo, n in HALVES:
+            scan(chg_s, chg, lo, n)
+        flip, half2 = tab(), tab()
+        steps = [lambda a=flip, b=chg_s: ts(a, picked(b), -2.0, col["one_2k"], A.mult, A.add), lambda a=half2, b=half, c=flip: tt(a, b, c, A.mult)]
 
         x2 = "xt%d" % (r + 1)
+        gather("a", plane(hg, 3, HALF, HALF), plane(h, 3), cols_of(tears, HALF, HALF))
         if not last:
-            gather("a", plane(hg, 3, HALF, HALF), plane(h, 3), part(tears, KT // 2, KT // 2))
+            k_half2, base = tab(), tab()
+            steps += [lambda a=k_half2, b=k_half, c=flip: tt(a, b, c, A.mult), lambda a=base, b=k_half2: tt(a, mid, b, A.subtract)]
+            half, k_half = half2, k_half2
             for b in range(3):
                 tt(vw(x2, b, C, 4), plane(h, b), plane(o, b), A.add, tears)
-            tt(vw(x2, 3, HALF, 4), plane(h, 3), plane(o, 3, 0, HALF), A.add, part(tears, 0, KT // 2))
+            tt(vw(x2, 3, HALF, 4), plane(h, 3), plane(o, 3, 0, HALF), A.add, cols_of(tears, 0, HALF))
             tt(vw(x2, 4 * HALF + 3, HALF, 4), part(own_f[3], HALF, HALF), plane(hg, 3, HALF, HALF), A.add)
     q, qs = "q3", "qs3"
-    for i in range(2):
-        lo = HALF * i
-        if i == 0:
-            gather("a", plane(hg, 3, HALF, HALF), plane(h, 3), part(tears, KT // 2, KT // 2))
-            xs = exchange(diff, base, chg_s)
-            d2, b2 = xs[5], xs[6]
-            lift, l0, l1, t0, t1 = tab(), tab(), tab(), off(), off()
-            steps = xs[:5] + [lambda: ts(lift, d2, col["k"], None, A.mult), lambda: tt(l0, lift, b2, A.add), lambda: tcopy(t0, l0),
-                              lambda: tt(l1, l0, d2, A.add), lambda: tcopy(t1, l1)]
+    l0, l1, t0, t1 = tab(), tab(), off(), off()
+    steps += [lambda: tt(l0, mid, half2, A.add), lambda: tt(l1, mid, half2, A.subtract), lambda: tcopy(t0, l0), lambda: tcopy(t1, l1)]
+    for i, (lo, n) in enumerate(HALVES):
         for b in range(4 - i):
-            tt(vw(x2, 4 * lo + b, HALF, 4), plane(h, b), plane(o, b, lo, HALF), A.add, part(tears, lo // 16, HALF // 16))
-            steps.pop(0)()
+            tt(vw(x2, 4 * lo + b, HALF, 4), plane(h, b), plane(o, b, lo, HALF), A.add, cols_of(tears, lo, HALF))
+            run(steps, 1 + (b > 1))
+        if i == 0:
+            for j, t in enumerate((t0, t1)):
+                gather("a", vw("lsr", C * j, C), vw("num", 0, C), t)
+            dma("a", T.ls[:, :], T.lsr[0:128:16, :], "out", 0, [vw("lsr", 0, 2 * C)], [])
         if i == 1:
-            for n, t in enumerate((t0, t1)):
-                gather("a", vw("lsr", C * n, C), vw("num", 0, C), t)
             tt(vw(x2, 4 * lo + 3, HALF, 4), part(own_f[3], lo, HALF), plane(hg, 3, lo, HALF), A.add)
         quant(q, qs, x2, lo, HALF)
         yb = mm((0, 7)[i], "qv", "qvs", 0, q, qs, lo, HALF)
@@ -453,12 +492,9 @@ def rank_program(g, core, T, topo):
         yv = vw("yt", lo, HALF)
         if i == 0:
             act(yv, yb)
-            for n in range(3):
-                steps.pop(0)()
         else:
             ts(yv, yb, 1.0, None, A.mult)
         dma("as"[i], T.y[:, lo:lo + HALF], ap(yv), "out", 0, [yv], [])
-    dma("a", T.ls[:, :], T.lsr[0:128:16, :], "out", 0, [vw("lsr", 0, 2 * C)], [])
     for sem in sorted(total):
         if known["g"].get(sem, 0) < total[sem]:
             g.wait_ge(T.sem[sem], total[sem])

@@ -26,7 +26,8 @@ SCRATCH = {
     "et8": ("sbuf", [128, 528], "bfloat16"), "qe8": ("sbuf", [128, 256], "float8_e4m3fn_x4"), "qe8s": ("sbuf", [128, 256], "uint8"),
     "mask": ("sbuf", [128, C], "bfloat16"), "ik": ("sbuf", [128, KT], "int32"), "ip": ("sbuf", [128, 8], "int32"),
     "cols": ("sbuf", [128, 16], "float32"), "plist": ("sbuf", [128, 8], "uint16"),
-    "num": ("sbuf", [128, C], "float32"), "lsr": ("sbuf", [128, 2 * C], "float32"), "yt": ("sbuf", [128, C], "float32"),
+    "xi": ("sbuf", [128, 2 * C], "bfloat16"), "pm": ("sbuf", [128, 2 * C], "float16"),
+    "num": ("sbuf", [128, 2 * C], "float32"), "lsr": ("sbuf", [128, 2 * C], "float32"), "yt": ("sbuf", [128, C], "float32"),
     "rows": ("sbuf", [128, C * (3 * ROWS + 1)], "bfloat16"), "sc": ("sbuf", [128, C * SLOTS], "float16"),
     "tf": ("sbuf", [128, KT * 3 * TABS], "float32"), "tu": ("sbuf", [128, KT * 3 * SLOTS], "uint16"),
     "te": ("sbuf", [128, 2 * KT], "float32"),
@@ -90,7 +91,7 @@ def rank_program(g, core, T, topo):
             for a2, b2, st2, w2, k2, tok in log.get(name, ()):
                 if k2 == kind and kind != "dma" and not (w2 and not w):
                     continue
-                if not bank and (b2 <= a or b <= a2 or not (w or w2) or (st == st2 and st > 1 and (a - a2) % st)):
+                if not bank and (b2 - st2 < a or b - st < a2 or not (w or w2) or (st == st2 and st > 1 and (a - a2) % st)):
                     continue
                 if tok[0] not in deps or deps[tok[0]][1] < tok[1]:
                     deps[tok[0]] = tok
@@ -142,9 +143,11 @@ def rank_program(g, core, T, topo):
             return tcopy(out, in_)
         do("g", lambda: g.affine_select(ap(out), ap(in_), [[0, out[2] - out[1]]], A.is_gt, 0.0, 1, 0), [in_], [out])
 
-    def gather(q, out, win, off):
+    def gather(q, out, win, off, scale=None):
         if q == "v":
             do("v", lambda: g.vector.tensor_copy(ap(out), ap(win).indirect(ap(off))), [win, off], [out])
+        elif scale:
+            do("a", lambda: g.scalar.activation(ap(out), ap(win).indirect(ap(off)), F.Copy, scale=scale), [win, off], [out])
         else:
             do("a", lambda: g.scalar.activation(ap(out), ap(win).indirect(ap(off)), F.Copy), [win, off], [out])
 
@@ -201,16 +204,16 @@ def rank_program(g, core, T, topo):
     def picked(s, lo=0, n=C):
         return vw("sc", s + lo + 15, n // 16, 16)
 
-    col = {k: vw("cols", i, 1) for i, k in enumerate(("p15", "z", "k", "turn", "one_2k"))}
+    col = {k: vw("cols", i, 1) for i, k in enumerate(("p15", "z", "k", "turn", "one_2k", "odd"))}
 
     def turn(o, s, lo=0, n=C):
         ts(cols_of(o, lo, n), picked(s, lo, n), col["turn"], None, A.add)
 
-    dma("s", T.xt0[:, 0:2 * C], T.x[:, 0:2 * C], "dx0", 16, [], [vw("xt0", 0, 2 * C)])
-    dma("a", T.ut[:, :], T.u[:, :], "du", 16, [], [vw("ut", 0, 512)])
-    dma("s", T.xt0[:, 2 * C:4 * C], T.x[:, 2 * C:4 * C], "dx1", 16, [], [vw("xt0", 2 * C, 2 * C)])
     dma("a", T.lai[:, :], T.la[:, :], "dl", 32, [], [vw("lai", 0, KT)])
-    dma("a", T.lbi[:, :], T.lb[:, :], "dl", 32, [], [vw("lbi", 0, KT)])
+    dma("s", T.lbi[:, :], T.lb[:, :], "dl", 32, [], [vw("lbi", 0, KT)])
+    dma("a", T.ut[:, :], T.u[:, :], "du", 16, [], [vw("ut", 0, 512)])
+    dma("s", T.xt0[:, 0:2 * C], T.x[:, 0:2 * C], "dx0", 16, [], [vw("xt0", 0, 2 * C)])
+    dma("s", T.xt0[:, 2 * C:4 * C], T.x[:, 2 * C:4 * C], "dx1", 16, [], [vw("xt0", 2 * C, 2 * C)])
     wait("s", ("dx0", 16, {}))
     wait("s", ("dx1", 16, {}))
     dma("s", T.wq[:, :].bitcast(dt.uint8), T.wc[:, :], "dw", 32, [], [vw("wq", 0, 512)])
@@ -219,12 +222,13 @@ def rank_program(g, core, T, topo):
 
     W = 48
     do("g", lambda: g.iota(T.im[:, :], [[1, W]], 128, -1), [], [vw("im", 0, W)])
+    do("g", lambda: g.iota(T.ip[:, :], [[16, 8]], 0, 0), [], [vw("ip", 0, 8)])
+    do("g", lambda: g.iota(T.num[:, :], [[1, 2 * C]], -C, 0, allow_small_or_imprecise_dtypes=True), [], [vw("num", 0, 2 * C)])
+    do("v", lambda: g.vector.memset(T.xi[:, :], 0.0), [], [vw("xi", 0, 2 * C)])
     do("v", lambda: g.vector.memset(T.ones[:, :], 1.0), [], [vw("ones", 0, 528)])
     do("g", lambda: g.affine_select(T.et[:, :], T.ones[:, :], [[-1, 528]], A.is_equal, 0.0, 8, 4), [vw("ones", 0, 528)], [vw("et", 0, 528)])
-    do("g", lambda: g.iota(T.ip[:, :], [[16, 8]], 0, 0), [], [vw("ip", 0, 8)])
     do("g", lambda: g.iota(T.ik[:, :], [[16, KT]], 0, 0), [], [vw("ik", 0, KT)])
     ident = row()
-    do("g", lambda: g.iota(ap(rv(ident)), [[1, C]], -int(MID), 0, allow_small_or_imprecise_dtypes=True), [], [rv(ident)])
     im2 = vw("im2", 0, W)
     first = vw("im2", 0, 1)
     ts(im2, vw("im", 0, W), 15, None, A.bitwise_and)
@@ -240,26 +244,29 @@ def rank_program(g, core, T, topo):
     tcopy(vw(mask, 2 * W, 2 * W), vw(mask, 0, 2 * W))
     ts(col["one_2k"], col["k"], 2.0, 1.0, A.mult, A.add)
     tcopy(vw(mask, 4 * W, 4 * W), vw(mask, 0, 4 * W))
-    act(vw("et8", 0, 528), vw("et", 0, 528), 0.125)
-    num_t, low_t, k_t = tab(), tab(), tab()
-    for b in range(4):
-        quant("qe", "qes", "et", 128 * b, 128, 8 - b)
     tcopy(vw("plist", 0, 8), vw("ip", 0, 8))
+    ts(col["odd"], col["turn"], 2.0, 1.0, A.mult, A.add)
+    num_t, low_t, gap, both_l = tab(), tab(), tab(), tab()
+    o_gap, o_sum = off(), off()
+
+    def spread(o, at):
+        gather("a", vw("pm", at, C, 2), vw("num", 0, 2 * C), o, 0.5)
+
+    tt(gap, vw("lai", 0, KT), vw("lbi", 0, KT), A.subtract)
+    tt(both_l, vw("lai", 0, KT), vw("lbi", 0, KT), A.add)
+    ts(o_gap, gap, float(C), None, A.add)
+    tcopy(o_sum, both_l)
+    spread(o_gap, 0)
     quant("qu", "qus", "ut", 0, 128)
-    ts(num_t, vw("ik", 0, KT), col["p15"], None, A.add)
     do("v", lambda: g.vector.tensor_copy(T.qr[:, :].bitcast(dt.uint32), T.qu[:, :].bitcast(dt.uint32).indirect(T.plist[:, 0:8])), [vw("qu", 0, 128), vw("plist", 0, 8)], [vw("qr", 0, 128)])
     do("a", lambda: g.scalar.activation(T.qrs[:, :], T.qus[:, :].indirect(T.plist[:, 0:8]), F.Copy), [vw("qus", 0, 128), vw("plist", 0, 8)], [vw("qrs", 0, 128)])
-    ts(low_t, num_t, -MID, col["k"], A.add, A.add)
-    ts(k_t, vw("ik", 0, KT), HALF, col["k"], A.is_ge, A.add)
+    spread(o_sum, 1)
     for b in range(2):
-        quant("qe8", "qe8s", "et8", 128 * b, 128, 6 - b)
-    whole, mid, half, k_half, base = tab(), tab(), tab(), tab(), tab()
-    steps = [lambda: tt(whole, vw("lai", 0, KT), vw("lbi", 0, KT), A.subtract), lambda: ts(half, whole, 0.5, None, A.mult),
-             lambda: tt(mid, half, vw("lbi", 0, KT), A.add), lambda: tt(k_half, half, k_t, A.mult), lambda: tt(base, mid, k_half, A.subtract)]
+        quant("qe", "qes", "et", 128 * b, 128, 8 - b)
 
     S_BANK = (0, 7)
     HALVES = ((0, HALF), (HALF, HALF))
-    CUTS = ((0, CUT), (CUT, C - CUT))
+    THIRDS = ((0, 128), (128, 128), (256, 128))
 
     def run(steps, n):
         for _ in range(min(n, len(steps))):
@@ -289,28 +296,37 @@ def rank_program(g, core, T, topo):
         for i in range(2):
             quant(q, qs, xt, HALF * i, HALF)
             sv.append(mm(S_BANK[i], "qr", "qrs", 0, q, qs, HALF * i, HALF))
-            if r == 0:
-                run(steps, 1)
         send(dst, vw(lq, 0, C), vw(q, 0, C), "aq%d" % r, True)
         send(dst, vw(lp, 0, C), vw(qs, 0, C), "aq%d" % r)
         if r == 0:
-            do("g", lambda: g.iota(T.num[:, :], [[1, C]], 0, 0, allow_small_or_imprecise_dtypes=True), [], [vw("num", 0, C)])
+            do("g", lambda: g.iota(ap(rv(ident)), [[1, C]], -int(MID), 0, allow_small_or_imprecise_dtypes=True), [], [rv(ident)])
+            for b in range(2, 4):
+                quant("qe", "qes", "et", 128 * b, 128, 8 - b)
         own_f = [mm(5 + b, "qe", "qes", 128 * b, q, qs, 0, C) for b in range(2)]
-        side = row()
-        do("a", lambda: g.scalar.activation(ap(rv(side, 0, HALF)), ap(sv[0]), F.Sign, bias=TINY), [sv[0]], [rv(side, 0, HALF)])
-        act(vw(sf, 0, HALF), sv[0])
-        run(steps, len(steps) - 1)
-        ts(rv(side, HALF, HALF), sv[1], 0.0, 2.0, A.is_ge, A.mult)
-        act(vw(sf, HALF, HALF), sv[1])
-        run(steps, 1)
-        s = place("sc", C)
-        scan(s, side, 0, C)
-        w, pair = tab(), place("tf", 2 * KT)
+        wide, twin, p_s, t_k = place("rows", 2 * C), row(), place("sc", C), off()
+        for i, (lo, n) in enumerate(HALVES):
+            side = vw("xi", 2 * lo + 1, n, 2)
+            do("a", lambda: g.scalar.activation(ap(side), ap(sv[i]), F.Sign, bias=TINY), [sv[i]], [side])
+            scan_of(rv(wide, 2 * lo, 2 * n), vw("xi", 2 * lo, 2 * n), vw("pm", 2 * lo, 2 * n), A.mult, A.add)
+        if r == 0:
+            act(vw("et8", 0, 528), vw("et", 0, 528), 0.125)
+        for i, (lo, n) in enumerate(HALVES):
+            act(vw(sf, lo, n), sv[i])
+        chosen = [vw("rows", wide + 2 * lo + 1, n, 2) for lo, n in HALVES]
+        for i, (lo, n) in enumerate(HALVES):
+            scan_of(vw("sc", p_s + lo, n), vw(mask, lo, n), chosen[i], A.add, A.max)
+            if i == 0:
+                tcopy(rv(twin, lo, n), chosen[i])
+        for i, (lo, n) in enumerate(HALVES):
+            ts(cols_of(t_k, lo, n), picked(p_s, lo, n), 2.0, col["odd"], A.mult, A.add)
+            if i == 0:
+                tcopy(rv(twin, HALF, HALF), chosen[1])
+        if r == 0:
+            for b in range(2):
+                quant("qe8", "qe8s", "et8", 128 * b, 128, 6 - b)
+            ts(num_t, vw("ik", 0, KT), col["p15"], None, A.add)
+        pair = place("tf", 2 * KT)
         to_self, p_t = vw("tf", pair, KT, 2), vw("tf", pair + 1, KT, 2)
-        tt(w, picked(s), half, A.mult)
-        tt(p_t, w, base, A.add)
-        t_k = off()
-        tcopy(t_k, p_t)
 
         def unpack_own(k):
             b, lo = k // 2, HALF * (k % 2)
@@ -328,51 +344,64 @@ def rank_program(g, core, T, topo):
             act(plane(out, b, lo, n), part(fp[b], lo, n), 0.125 if b < 2 else 1.0)
 
         spare = [lambda k=k: unpack_own(k) for k in range(7)] + [lambda lo=lo: unpack_src(0, f, lo, HALF) for lo in (0, HALF)]
-        run(spare, OPT.get("early", 2))
-        at = row()
-        for qq, (lo, n) in zip("va", HALVES):
-            gather(qq, rv(at, lo, n), rv(ident), cols_of(t_k, lo, n))
+        run(spare, OPT.get("early", 1))
 
-        low, twin = at, row()
-        tcopy(rv(twin), rv(at))
-        behind = None
+        at = low = rv(wide, 0, 2 * C)
+        behind = []
         for k in range(7):
             at2, low2, twin2, t2 = row(), row(), row(), off()
             ss = place("sc", C)
-            for i in range(2):
-                (lo, n), (lo2, n2) = HALVES[i], CUTS[i]
-                gather("a", rv(at2, lo, n), rv(at), cols_of(t_k, lo, n))
-                if i == 0 and behind:
-                    behind()
-                if i == 1:
-                    run(spare, 1)
-                if k == 0 and i == 0:
-                    tt(rv(low2, lo2, n2), rv(low), rv(twin, lo2, n2), A.min, cols_of(t_k, lo2, n2))
-                    scan(ss, at2, lo, n)
-                    tt(to_self, num_t, p_t, A.subtract)
+
+            def lower(j):
+                lo, n = THIRDS[j]
+                tt(rv(low2, lo, n), low, rv(twin, lo, n), A.min, cols_of(t_k, lo, n))
+                if j == 0 or j == 1 and k < 6:
+                    copy_on("g", rv(twin2, lo, n), rv(low2, lo, n))
                 else:
-                    scan(ss, at2, lo, n)
-                    tt(rv(low2, lo2, n2), rv(low), rv(twin, lo2, n2), A.min, cols_of(t_k, lo2, n2))
-                if i == 0:
-                    copy_on(OPT.get("tw", "g"), rv(twin2, lo2, n2), rv(low2, lo2, n2))
-                else:
-                    behind = lambda a=twin2, b=low2, lo=lo2, n=n2: copy_on("a", rv(a, lo, n), rv(b, lo, n))
+                    behind.append(lambda a=twin2, b=low2: copy_on("a", rv(a, lo, n), rv(b, lo, n)))
+
+            for lo, n in HALVES:
+                gather("a", rv(at2, lo, n), at, cols_of(t_k, lo, n))
+            run(behind, 1)
+            run(spare, 1)
+            if k == 0:
+                lower(0)
+            for i, (lo, n) in enumerate(HALVES):
+                scan(ss, at2, lo, n)
+                lower(i + (k == 0))
                 turn(t2, ss, lo, n)
-            at, low, twin, t_k = at2, low2, twin2, t2
-        behind()
+            if k > 0:
+                lower(2)
+            elif r == 0:
+                ts(low_t, num_t, -MID, col["k"], A.add, A.add)
+            at, low, twin, t_k = rv(at2), rv(low2), twin2, t2
+        run(behind, 2)
         run(spare, 9)
+        ts(p_t, picked(p_s), col["turn"], None, A.add)
         far, m = row(), row()
-        for lo, n in CUTS:
-            tt(rv(far, lo, n), rv(low), rv(twin, lo, n), A.min, cols_of(t_k, lo, n))
+
+        def lowest(j):
+            lo, n = THIRDS[j]
+            tt(rv(m, lo, n), rv(far), part(low, lo, n), A.min, cols_of(t_k, lo, n))
+
+        for j in OPT.get("fo", (1, 2, 0)):
+            lo, n = THIRDS[j]
+            tt(rv(far, lo, n), low, rv(twin, lo, n), A.min, cols_of(t_k, lo, n))
         unpack_src(1, f, 0, C)
         copy_on("g", plane(fd, 0), plane(f, 0))
         for b in range(2, 4):
             unpack_src(b, f, 0, C)
         unpack_src(1, fd, 0, C)
         s = place("sc", C)
-        tt(rv(m, 0, 128), rv(far), rv(low, 0, 128), A.min, cols_of(t_k, 0, 128))
         scan(s, far, 128, C - 128)
+        tt(to_self, num_t, p_t, A.subtract)
+        lowest(0)
+        e = OPT.get("mfill", 1)
+        if e:
+            lowest(1)
         scan(s, m, 0, 128)
+        if e:
+            lowest(2)
         both, tears = place("tf", 2 * KT), off()
         tt(vw("te", 1, KT, 2), picked(s), low_t, A.is_equal)
         scan_of(vw("tf", both, 2 * KT), vw("te", 0, 2 * KT), vw("tf", pair, 2 * KT), A.mult, A.add)
@@ -384,8 +413,8 @@ def rank_program(g, core, T, topo):
         for j, (out, win) in enumerate(((tr, ident), (tr2, tr))):
             for qq, (lo, n) in zip("va", HALVES):
                 gather(qq, rv(out, lo, n), rv(win), cols_of(tears, lo, n))
-            lo = 128 * (j + 1)
-            tt(rv(m, lo, 128), rv(far), rv(low, lo, 128), A.min, cols_of(t_k, lo, 128))
+            if not e:
+                lowest(j + 1)
         s = place("sc", C)
         scan(s, tr2, 0, C)
         if r == 0:
@@ -442,7 +471,8 @@ def rank_program(g, core, T, topo):
         for lo, n in HALVES:
             gather("a", vw(sr, lo, n), vw(sf, 0, C), cols_of(t_r, lo, n))
         z3(2)
-        z3(3)
+        for lo, n in HALVES:
+            tt(vw(zt, 4 * lo + 3, n, 4), plane(zb, 3), plane(zbd, 3, lo, n), A.add, cols_of(got4, lo, n))
         zq, zp = "zq%d" % r, "zp%d" % r
         chg = row()
         for i in range(2):
@@ -457,29 +487,31 @@ def rank_program(g, core, T, topo):
             tt(rv(chg, lo, n), sv[i], vw(sr, lo, n), A.is_lt)
         for lo, n in HALVES:
             scan(chg_s, chg, lo, n)
-        flip, half2 = tab(), tab()
-        steps = [lambda a=flip, b=chg_s: ts(a, picked(b), -2.0, col["one_2k"], A.mult, A.add), lambda a=half2, b=half, c=flip: tt(a, b, c, A.mult)]
+        flip, gap2 = tab(), tab()
+        ts(flip, picked(chg_s), -2.0, col["one_2k"], A.mult, A.add)
+        steps = [lambda: tt(gap2, gap, flip, A.mult)]
 
         x2 = "xt%d" % (r + 1)
         gather("a", plane(hg, 3, HALF, HALF), plane(h, 3), cols_of(tears, HALF, HALF))
         if not last:
-            k_half2, base = tab(), tab()
-            steps += [lambda a=k_half2, b=k_half, c=flip: tt(a, b, c, A.mult), lambda a=base, b=k_half2: tt(a, mid, b, A.subtract)]
-            half, k_half = half2, k_half2
+            o_gap = off()
+            steps += [lambda: ts(o_gap, gap2, float(C), None, A.add), lambda: spread(o_gap, 0)]
             for b in range(3):
                 tt(vw(x2, b, C, 4), plane(h, b), plane(o, b), A.add, tears)
+                run(steps, 1)
+            gap = gap2
             tt(vw(x2, 3, HALF, 4), plane(h, 3), plane(o, 3, 0, HALF), A.add, cols_of(tears, 0, HALF))
             tt(vw(x2, 4 * HALF + 3, HALF, 4), part(own_f[3], HALF, HALF), plane(hg, 3, HALF, HALF), A.add)
     q, qs = "q3", "qs3"
     l0, l1, t0, t1 = tab(), tab(), off(), off()
-    steps += [lambda: tt(l0, mid, half2, A.add), lambda: tt(l1, mid, half2, A.subtract), lambda: tcopy(t0, l0), lambda: tcopy(t1, l1)]
+    steps += [lambda: tt(l0, both_l, gap2, A.add), lambda: tt(l1, both_l, gap2, A.subtract), lambda: ts(t0, l0, 0.5, None, A.mult), lambda: ts(t1, l1, 0.5, None, A.mult)]
     for i, (lo, n) in enumerate(HALVES):
         for b in range(4 - i):
             tt(vw(x2, 4 * lo + b, HALF, 4), plane(h, b), plane(o, b, lo, HALF), A.add, cols_of(tears, lo, HALF))
-            run(steps, 1 + (b > 1))
+            run(steps, 1 + b % 2)
         if i == 0:
             for j, t in enumerate((t0, t1)):
-                gather("a", vw("lsr", C * j, C), vw("num", 0, C), t)
+                gather("a", vw("lsr", C * j, C), vw("num", C, C), t)
             dma("a", T.ls[:, :], T.lsr[0:128:16, :], "out", 0, [vw("lsr", 0, 2 * C)], [])
         if i == 1:
             tt(vw(x2, 4 * lo + 3, HALF, 4), part(own_f[3], lo, HALF), plane(hg, 3, lo, HALF), A.add)

@@ -5,10 +5,9 @@ C = 384
 HALF = C // 2
 STEPS = [1, 2, 3]
 KT = C // 16
-KH = KT // 2
-CUT = 192
-ROWS = 34
-SLOTS = 14
+PAD = 16
+ROWS = 37
+SLOTS = 16
 TABS = 20
 BIG, LIFT, MID = 2048.0, 512.0, 192.0
 TINY = 2.0 ** -100
@@ -26,19 +25,21 @@ SCRATCH = {
     "et8": ("sbuf", [128, 528], "bfloat16"), "qe8": ("sbuf", [128, 256], "float8_e4m3fn_x4"), "qe8s": ("sbuf", [128, 256], "uint8"),
     "mask": ("sbuf", [128, C], "bfloat16"), "ik": ("sbuf", [128, KT], "int32"), "ip": ("sbuf", [128, 8], "int32"),
     "cols": ("sbuf", [128, 16], "float32"), "plist": ("sbuf", [128, 8], "uint16"),
-    "xi": ("sbuf", [128, 2 * C], "bfloat16"), "pm": ("sbuf", [128, 2 * C], "float16"),
-    "num": ("sbuf", [128, 2 * C], "float32"), "lsr": ("sbuf", [128, 2 * C], "float32"), "yt": ("sbuf", [128, C], "float32"),
+    "xi": ("sbuf", [128, 3 * C], "bfloat16"), "pm": ("sbuf", [128, 3 * C], "float16"),
+    "num": ("sbuf", [128, 2 * C], "float32"), "lsr": ("sbuf", [128, C], "float32"), "yt": ("sbuf", [128, C], "float32"),
     "rows": ("sbuf", [128, C * (3 * ROWS + 1)], "bfloat16"), "sc": ("sbuf", [128, C * SLOTS], "float16"),
     "tf": ("sbuf", [128, KT * 3 * TABS], "float32"), "tu": ("sbuf", [128, KT * 3 * SLOTS], "uint16"),
-    "te": ("sbuf", [128, 2 * KT], "float32"),
+    "big": ("sbuf", [128, 2 * C], "bfloat16"),
+    "te": ("sbuf", [128, 2 * KT], "float32"), "zb": ("sbuf", [128, 8 * C], "bfloat16"), "alt": ("sbuf", [128, 2 * C], "bfloat16"),
 }
 for r in range(4):
     SCRATCH["xt%d" % r] = ("sbuf", [128, 4 * C], "bfloat16")
     SCRATCH["q%d" % r] = ("sbuf", [128, C], "float8_e4m3fn_x4")
     SCRATCH["qs%d" % r] = ("sbuf", [128, C], "uint8")
 for r in range(3):
-    for k in ("f", "zt", "h", "o"):
+    for k in ("f", "h", "o"):
         SCRATCH["%s%d" % (k, r)] = ("sbuf", [128, 4 * C], "bfloat16")
+    SCRATCH["zt%d" % r] = ("sbuf", [128, PAD + 4 * C], "bfloat16")
     for k in ("lq", "zq"):
         SCRATCH["%s%d" % (k, r)] = ("sbuf", [128, C], "float8_e4m3fn_x4")
     for k in ("lp", "zp"):
@@ -47,7 +48,7 @@ for r in range(3):
     SCRATCH["t2l%d" % r] = ("sbuf", [128, 2 * KT], "uint16")
     for k in ("sf", "sr"):
         SCRATCH["%s%d" % (k, r)] = ("sbuf", [128, C], "float32")
-for k in ("fd", "za", "zad", "zb", "zbd"):
+for k in ("fd", "za", "zad", "zi", "zbd"):
     SCRATCH[k] = ("sbuf", [128, 4 * C], "bfloat16")
 for r in range(8):
     SCRATCH["pb%d" % r] = ("psum", [128, 512], "float32")
@@ -141,7 +142,7 @@ def rank_program(g, core, T, topo):
             return act(out, in_)
         if q == "v":
             return tcopy(out, in_)
-        do("g", lambda: g.affine_select(ap(out), ap(in_), [[0, out[2] - out[1]]], A.is_gt, 0.0, 1, 0), [in_], [out])
+        do("g", lambda: g.affine_select(ap(out), ap(in_), [[0, (in_[2] - in_[1]) // in_[3]]], A.is_gt, 0.0, 1, 0), [in_], [out])
 
     def gather(q, out, win, off, scale=None):
         if q == "v":
@@ -198,79 +199,87 @@ def rank_program(g, core, T, topo):
     def scan_of(o, d0, d1, op0, op1):
         do("v", lambda: g.vector.tensor_tensor_scan(ap(o), ap(d0), ap(d1), 0.0, op0, op1), [d0, d1], [o])
 
-    def scan(out, a, lo, n):
-        scan_of(vw("sc", out + lo, n), vw(mask, lo, n), rv(a, lo, n), A.add, A.max)
+    def scan(out, a, lo=0, n=C):
+        scan_of(vw("sc", out + lo, n), vw(mask, lo, n), a if isinstance(a, tuple) else rv(a, lo, n), A.add, A.max)
 
     def picked(s, lo=0, n=C):
         return vw("sc", s + lo + 15, n // 16, 16)
 
-    col = {k: vw("cols", i, 1) for i, k in enumerate(("p15", "z", "k", "turn", "one_2k", "odd"))}
+    col = {k: vw("cols", i, 1) for i, k in enumerate(("p15", "z", "k", "turn", "one_2k", "third", "odd", "sign"))}
 
     def turn(o, s, lo=0, n=C):
         ts(cols_of(o, lo, n), picked(s, lo, n), col["turn"], None, A.add)
+
+    def run(steps, n=99):
+        for _ in range(min(n, len(steps))):
+            steps.pop(0)()
 
     dma("a", T.lai[:, :], T.la[:, :], "dl", 32, [], [vw("lai", 0, KT)])
     dma("s", T.lbi[:, :], T.lb[:, :], "dl", 32, [], [vw("lbi", 0, KT)])
     dma("a", T.ut[:, :], T.u[:, :], "du", 16, [], [vw("ut", 0, 512)])
     dma("s", T.xt0[:, 0:2 * C], T.x[:, 0:2 * C], "dx0", 16, [], [vw("xt0", 0, 2 * C)])
     dma("s", T.xt0[:, 2 * C:4 * C], T.x[:, 2 * C:4 * C], "dx1", 16, [], [vw("xt0", 2 * C, 2 * C)])
-    wait("s", ("dx0", 16, {}))
-    wait("s", ("dx1", 16, {}))
-    dma("s", T.wq[:, :].bitcast(dt.uint8), T.wc[:, :], "dw", 32, [], [vw("wq", 0, 512)])
-    dma("s", T.wp[:, :], T.ws[:, :], "dw", 32, [], [vw("wp", 0, 512)])
-    dma("s", T.vt[:, :], T.v[:, :], "dv", 16, [], [vw("vt", 0, 512)])
 
     W = 48
     do("g", lambda: g.iota(T.im[:, :], [[1, W]], 128, -1), [], [vw("im", 0, W)])
     do("g", lambda: g.iota(T.ip[:, :], [[16, 8]], 0, 0), [], [vw("ip", 0, 8)])
     do("g", lambda: g.iota(T.num[:, :], [[1, 2 * C]], -C, 0, allow_small_or_imprecise_dtypes=True), [], [vw("num", 0, 2 * C)])
-    do("v", lambda: g.vector.memset(T.xi[:, :], 0.0), [], [vw("xi", 0, 2 * C)])
-    do("v", lambda: g.vector.memset(T.ones[:, :], 1.0), [], [vw("ones", 0, 528)])
+    def fill(v, x):
+        do("v", lambda: g.vector.memset(ap(v), x), [], [v])
+
+    fill(vw("ones", 0, 528), 1.0)
     do("g", lambda: g.affine_select(T.et[:, :], T.ones[:, :], [[-1, 528]], A.is_equal, 0.0, 8, 4), [vw("ones", 0, 528)], [vw("et", 0, 528)])
     do("g", lambda: g.iota(T.ik[:, :], [[16, KT]], 0, 0), [], [vw("ik", 0, KT)])
     ident = row()
     im2 = vw("im2", 0, W)
     first = vw("im2", 0, 1)
+    fill(vw("xi", 0, C, 3), 0.0)
     ts(im2, vw("im", 0, W), 15, None, A.bitwise_and)
-    do("v", lambda: g.vector.memset(T.te[:, :], 0.0), [], [vw("te", 0, 2 * KT)])
+    fill(vw("xi", 1, C, 3), 0.0)
     ts(vw("ma", 0, W), im2, 0, -BIG, A.is_equal, A.mult)
     ts(vw("mb", 0, W), im2, 1, LIFT, A.is_equal, A.mult)
-    ts(col["z"], first, 0, 16, A.not_equal, A.mult)
     ts(col["k"], first, 1, LIFT, A.not_equal, A.mult)
+    tcopy(vw("pm", 0, C, 3), vw("xi", 0, C, 3))
     tt(vw(mask, 0, W), vw("ma", 0, W), vw("mb", 0, W), A.add)
-    tt(col["p15"], col["z"], first, A.subtract)
-    tcopy(vw(mask, W, W), vw(mask, 0, W))
     ts(col["turn"], col["k"], -1.0, MID, A.mult, A.add)
-    tcopy(vw(mask, 2 * W, 2 * W), vw(mask, 0, 2 * W))
-    ts(col["one_2k"], col["k"], 2.0, 1.0, A.mult, A.add)
-    tcopy(vw(mask, 4 * W, 4 * W), vw(mask, 0, 4 * W))
     tcopy(vw("plist", 0, 8), vw("ip", 0, 8))
-    ts(col["odd"], col["turn"], 2.0, 1.0, A.mult, A.add)
+    ts(col["z"], first, 0, 16, A.not_equal, A.mult)
+    tcopy(vw(mask, W, W), vw(mask, 0, W))
     num_t, low_t, gap, both_l = tab(), tab(), tab(), tab()
     o_gap, o_sum = off(), off()
 
-    def spread(o, at):
-        gather("a", vw("pm", at, C, 2), vw("num", 0, 2 * C), o, 0.5)
+    def spread(o, at, scale):
+        gather("a", vw("pm", at, C, 3), vw("num", 0, 2 * C), o, scale)
 
     tt(gap, vw("lai", 0, KT), vw("lbi", 0, KT), A.subtract)
     tt(both_l, vw("lai", 0, KT), vw("lbi", 0, KT), A.add)
+    tcopy(vw(mask, 2 * W, 2 * W), vw(mask, 0, 2 * W))
+    ts(col["third"], col["turn"], 3.0, 2.0, A.mult, A.add)
     ts(o_gap, gap, float(C), None, A.add)
     tcopy(o_sum, both_l)
-    spread(o_gap, 0)
+    tcopy(vw(mask, 4 * W, 4 * W), vw(mask, 0, 4 * W))
+    spread(o_gap, 1, 0.5)
     quant("qu", "qus", "ut", 0, 128)
+    tt(col["p15"], col["z"], first, A.subtract)
+    ts(col["one_2k"], col["k"], 2.0, 1.0, A.mult, A.add)
+    ts(col["odd"], col["turn"], 2.0, 1.0, A.mult, A.add)
+    ts(col["sign"], first, -0.25, 1.0, A.mult, A.add)
     do("v", lambda: g.vector.tensor_copy(T.qr[:, :].bitcast(dt.uint32), T.qu[:, :].bitcast(dt.uint32).indirect(T.plist[:, 0:8])), [vw("qu", 0, 128), vw("plist", 0, 8)], [vw("qr", 0, 128)])
     do("a", lambda: g.scalar.activation(T.qrs[:, :], T.qus[:, :].indirect(T.plist[:, 0:8]), F.Copy), [vw("qus", 0, 128), vw("plist", 0, 8)], [vw("qrs", 0, 128)])
-    spread(o_sum, 1)
-    for b in range(2):
-        quant("qe", "qes", "et", 128 * b, 128, 8 - b)
+    spread(o_sum, 2, 0.5)
+    fill(vw("te", 0, 2 * KT), 0.0)
+    fill(vw("big", 0, C, 2), BIG)
+    fill(vw("big", 1, C, 2), 0.0)
 
-    S_BANK = (0, 7)
     HALVES = ((0, HALF), (HALF, HALF))
     THIRDS = ((0, 128), (128, 128), (256, 128))
+    PIECES = ((0, 256), (256, 128))
+    around = [[], [], []]
 
-    def run(steps, n):
-        for _ in range(min(n, len(steps))):
-            steps.pop(0)()
+    def exchange(flags, gap):
+        s, flip, gap2 = place("sc", C), tab(), tab()
+        return [lambda i=i, lo=lo, n=n: scan(s, flags[i], lo, n) for i, (lo, n) in enumerate(HALVES)] + [
+            lambda: ts(flip, picked(s), -2.0, col["one_2k"], A.mult, A.add), lambda: tt(gap2, gap, flip, A.mult)], gap2
 
     for r, d in enumerate(STEPS):
         last = r == len(STEPS) - 1
@@ -279,8 +288,8 @@ def rank_program(g, core, T, topo):
         lq, lp, t1l, t2l = "lq%d" % r, "lp%d" % r, "t1l%d" % r, "t2l%d" % r
         src = T.cores[(me - d) % n_ranks]
         ne = len(topo.engines(src, core))
-        total["aq%d" % r], total["at%d" % r], total["au%d" % r], total["av%d" % r] = 2 * ne, ne, ne, ne
-        note("dma", [], [vw(lq, 0, C), vw(lp, 0, C)], ("aq%d" % r, 2 * ne, {}))
+        total["aq%d" % r], total["at%d" % r], total["au%d" % r], total["av%d" % r] = (2 + (r == 0)) * ne, ne, ne, ne
+        note("dma", [], [vw(lq, 0, C), vw(lp, 0, C)], ("aq%d" % r, total["aq%d" % r], {}))
         got1, got2, got4 = vw(t1l, 0, KT), vw(t2l, 0, KT), vw(t2l, KT, KT)
         for t, sem in ((got1, "at"), (got2, "au"), (got4, "av")):
             note("dma", [], [t], ("%s%d" % (sem, r), ne, {}))
@@ -288,40 +297,48 @@ def rank_program(g, core, T, topo):
         fd, za, zad, zb, zbd, hg = "fd", "za", "zad", "zb", "zbd", "zbd"
         sf, sr = "sf%d" % r, "sr%d" % r
         nxt["sc"] = 0
+        held, free = ((0, 7), (1, 2))[r % 2], ((1, 2), (0, 7))[r % 2]
 
         def plane(t, b, lo=0, n=C):
             return vw(t, C * b + lo, n)
 
         sv = []
         for i in range(2):
+            run(around[i])
             quant(q, qs, xt, HALF * i, HALF)
-            sv.append(mm(S_BANK[i], "qr", "qrs", 0, q, qs, HALF * i, HALF))
-        send(dst, vw(lq, 0, C), vw(q, 0, C), "aq%d" % r, True)
+            sv.append(mm(held[i], "qr", "qrs", 0, q, qs, HALF * i, HALF))
+            if r == 0:
+                send(dst, vw(lq, HALF * i, HALF), vw(q, HALF * i, HALF), "aq0", True)
+        run(around[2])
+        if r > 0:
+            send(dst, vw(lq, 0, C), vw(q, 0, C), "aq%d" % r, True)
         send(dst, vw(lp, 0, C), vw(qs, 0, C), "aq%d" % r)
         if r == 0:
+            wait("s", ("aq0", total["aq0"], {}))
+            dma("s", T.wq[:, :].bitcast(dt.uint8), T.wc[:, :], "dw", 32, [], [vw("wq", 0, 512)])
+            dma("s", T.wp[:, :], T.ws[:, :], "dw", 32, [], [vw("wp", 0, 512)])
+            dma("s", T.vt[:, :], T.v[:, :], "dv", 16, [], [vw("vt", 0, 512)])
             do("g", lambda: g.iota(ap(rv(ident)), [[1, C]], -int(MID), 0, allow_small_or_imprecise_dtypes=True), [], [rv(ident)])
-            for b in range(2, 4):
+            for b in range(4):
                 quant("qe", "qes", "et", 128 * b, 128, 8 - b)
         own_f = [mm(5 + b, "qe", "qes", 128 * b, q, qs, 0, C) for b in range(2)]
-        wide, twin, p_s, t_k = place("rows", 2 * C), row(), place("sc", C), off()
+        wide, twin, p_s, t_k = place("rows", 3 * C), place("rows", 2 * C), place("sc", C), off()
+        chosen = [vw("rows", wide + 3 * lo + 2, n, 3) for lo, n in HALVES]
         for i, (lo, n) in enumerate(HALVES):
-            side = vw("xi", 2 * lo + 1, n, 2)
+            side = vw("xi", 3 * lo + 2, n, 3)
             do("a", lambda: g.scalar.activation(ap(side), ap(sv[i]), F.Sign, bias=TINY), [sv[i]], [side])
-            scan_of(rv(wide, 2 * lo, 2 * n), vw("xi", 2 * lo, 2 * n), vw("pm", 2 * lo, 2 * n), A.mult, A.add)
         if r == 0:
             act(vw("et8", 0, 528), vw("et", 0, 528), 0.125)
         for i, (lo, n) in enumerate(HALVES):
             act(vw(sf, lo, n), sv[i])
-        chosen = [vw("rows", wide + 2 * lo + 1, n, 2) for lo, n in HALVES]
-        for i, (lo, n) in enumerate(HALVES):
-            scan_of(vw("sc", p_s + lo, n), vw(mask, lo, n), chosen[i], A.add, A.max)
-            if i == 0:
-                tcopy(rv(twin, lo, n), chosen[i])
-        for i, (lo, n) in enumerate(HALVES):
-            ts(cols_of(t_k, lo, n), picked(p_s, lo, n), 2.0, col["odd"], A.mult, A.add)
-            if i == 0:
-                tcopy(rv(twin, HALF, HALF), chosen[1])
-        if r == 0:
+        choose = [lambda lo=lo, n=n: scan_of(rv(wide, 3 * lo, 3 * n), vw("xi", 3 * lo, 3 * n), vw("pm", 3 * lo, 3 * n), A.mult, A.add) for lo, n in HALVES]
+        diag = [lambda i=i, lo=lo, n=n: scan(p_s, chosen[i], lo, n) for i, (lo, n) in enumerate(HALVES)]
+        copy = [lambda i=i, lo=lo, n=n: tcopy(vw("rows", twin + 2 * lo, n, 2), chosen[i]) for i, (lo, n) in enumerate(HALVES)]
+        offs = [lambda lo=lo, n=n: ts(cols_of(t_k, lo, n), picked(p_s, lo, n), 3.0, col["third"], A.mult, A.add) for lo, n in HALVES]
+        if r > 0:
+            run([choose[0], diag[0], choose[1], offs[0], copy[0], diag[1], copy[1], offs[1]])
+        else:
+            run([choose[0], choose[1], diag[0], copy[0], diag[1], offs[0], copy[1], offs[1]])
             for b in range(2):
                 quant("qe8", "qe8s", "et8", 128 * b, 128, 6 - b)
             ts(num_t, vw("ik", 0, KT), col["p15"], None, A.add)
@@ -340,15 +357,26 @@ def rank_program(g, core, T, topo):
         def unpack_src(b, out, lo, n):
             if len(fp) == b:
                 e, es, ea = ("qe", "qes", 128 * b) if b < 2 else ("qe8", "qe8s", 128 * (b - 2))
-                fp.append(mm(1 + b, e, es, ea, lq, lp, 0, C))
+                fp.append(mm((free + (3, 4))[b], e, es, ea, lq, lp, 0, C))
             act(plane(out, b, lo, n), part(fp[b], lo, n), 0.125 if b < 2 else 1.0)
 
-        spare = [lambda k=k: unpack_own(k) for k in range(7)] + [lambda lo=lo: unpack_src(0, f, lo, HALF) for lo in (0, HALF)]
-        run(spare, OPT.get("early", 1))
+        spare = [lambda k=k: unpack_own(k) for k in (0, 1, 2, 3, 4, 6)]
 
-        at = low = rv(wide, 0, 2 * C)
-        behind = []
-        for k in range(7):
+        low, twin2, ss, t2 = place("rows", 2 * C), row(), place("sc", C), off()
+        for lo, n in HALVES:
+            gather("a", vw("rows", twin + 2 * lo + 1, n, 2), rv(wide, 0, 3 * C), cols_of(t_k, lo, n))
+        run(spare, 1)
+        for i, (lo, n) in enumerate(HALVES):
+            scan(ss, vw("rows", twin + 2 * lo + 1, n, 2), lo, n)
+            scan_of(rv(low, 2 * lo, 2 * n), vw("big", 2 * lo, 2 * n), rv(twin, 2 * lo, 2 * n), A.add, A.min)
+            copy_on("g", rv(twin2, 128 * i, 128), vw("rows", low + 256 * i + 1, 128, 2))
+            ts(cols_of(t2, lo, n), picked(ss, lo, n), 2.0, col["odd"], A.mult, A.add)
+        if r == 0:
+            ts(low_t, num_t, -MID, col["k"], A.add, A.add)
+        behind = [lambda a=twin2, b=low: copy_on("a", rv(a, 256, 128), vw("rows", b + 513, 128, 2))]
+        at, low, twin, t_k = rv(twin, 0, 2 * C), rv(low, 0, 2 * C), twin2, t2
+        cut = THIRDS if OPT.get("p3") else HALVES
+        for k in range(1, 7):
             at2, low2, twin2, t2 = row(), row(), row(), off()
             ss = place("sc", C)
 
@@ -360,69 +388,77 @@ def rank_program(g, core, T, topo):
                 else:
                     behind.append(lambda a=twin2, b=low2: copy_on("a", rv(a, lo, n), rv(b, lo, n)))
 
-            for lo, n in HALVES:
+            for lo, n in cut:
                 gather("a", rv(at2, lo, n), at, cols_of(t_k, lo, n))
             run(behind, 1)
             run(spare, 1)
-            if k == 0:
-                lower(0)
-            for i, (lo, n) in enumerate(HALVES):
-                scan(ss, at2, lo, n)
-                lower(i + (k == 0))
-                turn(t2, ss, lo, n)
-            if k > 0:
-                lower(2)
-            elif r == 0:
-                ts(low_t, num_t, -MID, col["k"], A.add, A.add)
+            plan = OPT.get("p3", "s0 l0 t0 s1 l1 t1 l2") if k else OPT.get("p30", "l0 s0 l1 t0 s1 l2 t1")
+            if k == 6:
+                plan = OPT.get("p36", plan)
+            for w in plan.split():
+                j = int(w[1])
+                if w[0] == "l":
+                    lower(j)
+                elif w[0] == "s":
+                    scan(ss, at2, *cut[j])
+                else:
+                    turn(t2, ss, *cut[j])
             at, low, twin, t_k = rv(at2), rv(low2), twin2, t2
-        run(behind, 2)
-        run(spare, 9)
-        ts(p_t, picked(p_s), col["turn"], None, A.add)
-        far, m = row(), row()
+        far, m, at2, t2, ss, s = row(), row(), row(), off(8), place("sc", 128), place("sc", C)
+        both, tears = place("tf", 2 * KT), off()
+
+        def farther(j):
+            lo, n = THIRDS[j]
+            tt(rv(far, lo, n), low, rv(twin, lo, n), A.min, cols_of(t_k, lo, n))
 
         def lowest(j):
             lo, n = THIRDS[j]
             tt(rv(m, lo, n), rv(far), part(low, lo, n), A.min, cols_of(t_k, lo, n))
 
-        for j in OPT.get("fo", (1, 2, 0)):
-            lo, n = THIRDS[j]
-            tt(rv(far, lo, n), low, rv(twin, lo, n), A.min, cols_of(t_k, lo, n))
-        unpack_src(1, f, 0, C)
+        gather("a", rv(at2, 0, 128), at, cols_of(t_k, 0, 128))
+        run(behind)
+        unpack_src(0, f, 0, C)
         copy_on("g", plane(fd, 0), plane(f, 0))
-        for b in range(2, 4):
+        for b in range(1, 4):
             unpack_src(b, f, 0, C)
         unpack_src(1, fd, 0, C)
-        s = place("sc", C)
-        scan(s, far, 128, C - 128)
-        tt(to_self, num_t, p_t, A.subtract)
-        lowest(0)
-        e = OPT.get("mfill", 1)
-        if e:
-            lowest(1)
-        scan(s, m, 0, 128)
-        if e:
-            lowest(2)
-        both, tears = place("tf", 2 * KT), off()
-        tt(vw("te", 1, KT, 2), picked(s), low_t, A.is_equal)
-        scan_of(vw("tf", both, 2 * KT), vw("te", 0, 2 * KT), vw("tf", pair, 2 * KT), A.mult, A.add)
-        tcopy(tears, vw("tf", both + 1, KT, 2))
+        calls = {"p": lambda: ts(p_t, picked(p_s), col["turn"], None, A.add), "q": lambda: tt(to_self, num_t, p_t, A.subtract),
+                 "s": lambda: scan(ss, at2, 0, 128), "t": lambda: turn(t2, ss, 0, 128), "f0": lambda: farther(0), "f1": lambda: farther(1), "f2": lambda: farther(2),
+                 "m0": lambda: tt(rv(m, 0, 128), low, rv(far, 0, 128), A.min, t2), "m1": lambda: lowest(1), "m2": lambda: lowest(2),
+                 "d0": lambda: scan(s, m, 0, 128), "d1": lambda: scan(s, far, 128, 128), "d2": lambda: scan(s, part(low, 256, 128), 256, 128),
+                 "e": lambda: tt(vw("te", 1, KT, 2), picked(s), low_t, A.is_equal),
+                 "x": lambda: scan_of(vw("tf", both, 2 * KT), vw("te", 0, 2 * KT), vw("tf", pair, 2 * KT), A.mult, A.add),
+                 "c": lambda: tcopy(tears, vw("tf", both + 1, KT, 2))}
+        if r == 0:
+            steps = [lambda: fill(vw("alt", 0, C, 2), 0.0), lambda: fill(vw("alt", 1, C, 2), 1.0)]
+        else:
+            steps, gap = exchange([vw("xi", 3 * lo + 1, n, 3) for lo, n in HALVES], gap)
+            o_gap = off()
+            steps.append(lambda: ts(o_gap, gap, float(C), None, A.add))
+        calls["+"] = lambda: run(steps, 1)
+        for w in OPT.get("end", "p s + f0 t f1 m0 d2 d1 q d0 f2 e + x m1 c").split():
+            calls[w]()
         send(dst, got1, tears, "at%d" % r)
+
+        lead = [m, row(), row(), row()]
+
+        def follow(j):
+            gather("a", rv(lead[j + 1]), rv(lead[j]), t_k)
 
         tr, tr2, tr4 = row(), row(), row()
         jump2, jump4 = off(), off()
+        run(steps, 1)
         for j, (out, win) in enumerate(((tr, ident), (tr2, tr))):
             for qq, (lo, n) in zip("va", HALVES):
                 gather(qq, rv(out, lo, n), rv(win), cols_of(tears, lo, n))
-            if not e:
-                lowest(j + 1)
+            if j == 0:
+                lowest(2)
+        run(steps, 1)
         s = place("sc", C)
-        scan(s, tr2, 0, C)
-        if r == 0:
-            quant("qv", "qvs", "vt", 0, 128)
+        scan(s, tr2)
+        run(steps)
         turn(jump2, s)
         send(dst, got2, jump2, "au%d" % r)
-
-        lead = [m, row(), row(), row()]
 
         def z1(b):
             if b < 2:
@@ -430,103 +466,89 @@ def rank_program(g, core, T, topo):
             else:
                 tt(plane(za, b), fp[b], plane(fd, b), A.add)
 
+        shared = OPT.get("shared", (2, 3))
+
         def z2(b):
-            tt(plane(zb, b), plane(za, b), plane(zad, b), A.add, got2)
+            if b not in shared:
+                tt(vw(zb, 2 * C * b + 1, C, 2), plane(za, b), plane(zad, b), A.add, got2)
+            else:
+                scan_of(vw(zb, 2 * C * b, 2 * C), vw("alt", 0, 2 * C), vw("zi", 2 * C * (b - 2), 2 * C), A.mult, A.add)
 
-        def z3(b):
-            tt(vw(zt, b, C, 4), plane(zb, b), plane(zbd, b), A.add, got4)
+        def z3(b, lo=0, n=C):
+            tt(vw(zt, 4 * lo + b, n, 4), vw(zb, 2 * C * b, 2 * C), plane(zbd, b, lo, n), A.add, cols_of(got4, lo, n))
 
-        def follow(j):
-            gather("a", rv(lead[j + 1]), rv(lead[j]), t_k)
+        def beside(qq, b):
+            copy_on(qq, vw("zi", 2 * C * (b - 2), C, 2) if b in shared else plane(zad, b), plane(za, b))
 
-        if OPT.get("lead1", 1):
-            follow(0)
-        gather("a", plane(fd, 2), plane(f, 2), got1)
-        gather("a", rv(tr4), rv(tr2), jump2)
-        gather("a", plane(fd, 3), plane(f, 3), got1)
-        for b in range(3):
-            z1(b)
-            copy_on("gga"[b], plane(zad, b), plane(za, b))
-        s = place("sc", C)
-        scan(s, tr4, 0, C)
-        z2(0)
-        turn(jump4, s)
-        send(dst, got4, jump4, "av%d" % r)
-        z1(3)
-        copy_on("a", plane(zad, 3), plane(za, 3))
-        copy_on("g", plane(zbd, 0), plane(zb, 0))
-        if not OPT.get("lead1", 1):
-            follow(0)
-        follow(1)
-        for b in range(1, 4):
-            z2(b)
-            copy_on("aga"[b - 1], plane(zbd, b), plane(zb, b))
-            if b == 1:
-                follow(2)
-        z3(0)
-        s, t_r = place("sc", C), off()
-        scan(s, lead[3], 0, C)
-        z3(1)
-        turn(t_r, s)
-        for lo, n in HALVES:
-            gather("a", vw(sr, lo, n), vw(sf, 0, C), cols_of(t_r, lo, n))
-        z3(2)
-        for lo, n in HALVES:
-            tt(vw(zt, 4 * lo + 3, n, 4), plane(zb, 3), plane(zbd, 3, lo, n), A.add, cols_of(got4, lo, n))
+        s4, sp = place("sc", C), 256
+        calls = {"f": follow, "g": lambda b: gather("a", plane(fd, b), plane(f, b), got1), "t": lambda b: gather("a", rv(tr4), rv(tr2), jump2),
+                 "z": z1, "y": z2, "x": z3, "a": lambda b: beside("a", b), "b": lambda b: beside("g", b),
+                 "c": lambda b: copy_on("a", plane(zbd, b), vw(zb, 2 * C * b + 1, C, 2)), "d": lambda b: copy_on("g", plane(zbd, b), vw(zb, 2 * C * b + 1, C, 2)),
+                 "e": lambda b: gather("a", vw("zi", 2 * C * (b - 2) + 1, C, 2), plane(za, b), got2) if b in shared else None,
+                 "B": lambda b: copy_on("g", plane(zad, b, 0, sp), plane(za, b, 0, sp)), "h": lambda b: copy_on("a", plane(zad, b, sp, C - sp), plane(za, b, sp, C - sp)),
+                 "D": lambda b: copy_on("g", plane(zbd, b, 0, sp), vw(zb, 2 * C * b + 1, sp, 2)), "i": lambda b: copy_on("a", plane(zbd, b, sp, C - sp), vw(zb, 2 * C * b + 1 + 2 * sp, C - sp, 2)),
+                 "s": lambda b: scan(s4, tr4), "p": lambda b: (spread(o_gap, 1, 0.5) if r else None) if b else act(vw("pm", 0, C, 3), vw("pm", 1, C, 3), -2.0),
+                 "u": lambda b: (ts(jump4, picked(s4), 2.0, col["odd"], A.mult, A.add), send(dst, got4, jump4, "av%d" % r))}
+        for w in OPT.get("zplan", "f0 g2 t0 g3 z0 b0 z1 B1 z2 a2 e2 h1 s0 u0 z3 a3 e3 y0 d0 y1 c1 y2 D2 i2 y3 c3 f1 f2 p1 p0 x0 x1 x2").split():
+            calls[w[0]](int(w[1]))
         zq, zp = "zq%d" % r, "zp%d" % r
-        chg = row()
-        for i in range(2):
-            quant(zq, zp, zt, HALF * i, HALF)
-            hb = mm((1, 5)[i], "wq", "wp", 0, zq, zp, HALF * i, HALF)
-            act(plane(h, 0, HALF * i, HALF), hb, 0.03125)
-        for b in range(1, 4):
-            hb = mm(1 + b, "wq", "wp", 128 * b, zq, zp, 0, C)
-            act(plane(h, b), hb, 0.03125)
-        chg_s = place("sc", C)
+
+        def layer(bank, b, lo, n):
+            act(plane(h, b, lo, n), mm(bank, "wq", "wp", 128 * b, zq, zp, lo, n), 0.03125)
+
+        z3(3, 0, 256)
+        z3(3, 256, 128)
+        for i, (lo, n) in enumerate(THIRDS):
+            quant(zq, zp, zt, lo, n)
+            layer((free[0], free[1], 3)[i], 0, lo, n)
         for i, (lo, n) in enumerate(HALVES):
-            tt(rv(chg, lo, n), sv[i], vw(sr, lo, n), A.is_lt)
-        for lo, n in HALVES:
-            scan(chg_s, chg, lo, n)
-        flip, gap2 = tab(), tab()
-        ts(flip, picked(chg_s), -2.0, col["one_2k"], A.mult, A.add)
-        steps = [lambda: tt(gap2, gap, flip, A.mult)]
+            layer((4, free[0])[i], 1, lo, n)
+        layer(free[1], 2, 0, C)
+        layer(3, 3, 0, C)
+        s, t_r = place("sc", C), off()
+        scan(s, lead[3])
+        if r == 0:
+            quant("qv", "qvs", "vt", 0, 128)
+        if last:
+            ts(vw("xi", 2, C, 3), vw("xi", 0, C, 3), col["sign"], None, A.add)
+        turn(t_r, s)
 
         x2 = "xt%d" % (r + 1)
-        gather("a", plane(hg, 3, HALF, HALF), plane(h, 3), cols_of(tears, HALF, HALF))
-        if not last:
-            o_gap = off()
-            steps += [lambda: ts(o_gap, gap2, float(C), None, A.add), lambda: spread(o_gap, 0)]
-            for b in range(3):
-                tt(vw(x2, b, C, 4), plane(h, b), plane(o, b), A.add, tears)
-                run(steps, 1)
-            gap = gap2
-            tt(vw(x2, 3, HALF, 4), plane(h, 3), plane(o, 3, 0, HALF), A.add, cols_of(tears, 0, HALF))
-            tt(vw(x2, 4 * HALF + 3, HALF, 4), part(own_f[3], HALF, HALF), plane(hg, 3, HALF, HALF), A.add)
+        for b in (2, 3):
+            gather("a", plane(hg, b, HALF, HALF), plane(h, b), cols_of(tears, HALF, HALF))
+        for lo, n in HALVES:
+            gather("a", vw(sr, lo, n), vw(sf, 0, C), cols_of(t_r, lo, n))
+
+        def state(b, lo=0, n=C, x2=x2, h=h, o=o, tears=tears, kept=own_f):
+            if b >= 2 and lo == HALF:
+                tt(vw(x2, 4 * lo + b, n, 4), part(kept[b], lo, n), plane(hg, b, lo, n), A.add)
+            else:
+                tt(vw(x2, 4 * lo + b, n, 4), plane(h, b), plane(o, b, lo, n), A.add, cols_of(tears, lo, n))
+
+        compare = [lambda i=i, lo=lo, n=n, sv=sv, sr=sr: tt(vw("xi", 3 * lo + 1, n, 3), sv[i], vw(sr, lo, n), A.is_lt) for i, (lo, n) in enumerate(HALVES)]
+        state(0)
+        state(1)
+        state(2, 0, HALF)
+        state(3, 0, HALF)
+        around = [[lambda: state(2, HALF, HALF)], [lambda: state(3, HALF, HALF), compare[0]], [compare[1]]]
     q, qs = "q3", "qs3"
-    l0, l1, t0, t1 = tab(), tab(), off(), off()
-    steps += [lambda: tt(l0, both_l, gap2, A.add), lambda: tt(l1, both_l, gap2, A.subtract), lambda: ts(t0, l0, 0.5, None, A.mult), lambda: ts(t1, l1, 0.5, None, A.mult)]
+    ys = []
     for i, (lo, n) in enumerate(HALVES):
-        for b in range(4 - i):
-            tt(vw(x2, 4 * lo + b, HALF, 4), plane(h, b), plane(o, b, lo, HALF), A.add, cols_of(tears, lo, HALF))
-            run(steps, 1 + b % 2)
-        if i == 0:
-            for j, t in enumerate((t0, t1)):
-                gather("a", vw("lsr", C * j, C), vw("num", C, C), t)
-            dma("a", T.ls[:, :], T.lsr[0:128:16, :], "out", 0, [vw("lsr", 0, 2 * C)], [])
-        if i == 1:
-            tt(vw(x2, 4 * lo + 3, HALF, 4), part(own_f[3], lo, HALF), plane(hg, 3, lo, HALF), A.add)
-        quant(q, qs, x2, lo, HALF)
-        yb = mm((0, 7)[i], "qv", "qvs", 0, q, qs, lo, HALF)
-        qv = vw(q, lo, HALF)
-        dma("s", T.oc[:, 4 * lo:4 * lo + 4 * HALF], ap(qv).bitcast(dt.uint8), "out", 0, [qv], [])
-        for k in range(4):
-            dma("s", T.osc[4 * k:4 * k + 4, lo:lo + HALF], T[qs][32 * k:32 * k + 4, lo:lo + HALF], "out", 0, [vw(qs, lo, HALF)], [])
-        yv = vw("yt", lo, HALF)
-        if i == 0:
-            act(yv, yb)
-        else:
-            ts(yv, yb, 1.0, None, A.mult)
-        dma("as"[i], T.y[:, lo:lo + HALF], ap(yv), "out", 0, [yv], [])
+        run(around[i])
+        quant(q, qs, x2, lo, n)
+        ys.append(mm(free[i], "qv", "qvs", 0, q, qs, lo, n))
+        dma("s", T.oc[:, 4 * lo:4 * lo + 4 * n], ap(vw(q, lo, n)).bitcast(dt.uint8), "out", 0, [vw(q, lo, n)], [])
+    for k in range(4):
+        dma("saaa"[k], T.osc[4 * k:4 * k + 4, :], T[qs][32 * k:32 * k + 4, :], "out", 0, [vw(qs, 0, C)], [])
+    run(around[2])
+    wide = place("rows", 3 * C)
+    for i, (lo, n) in enumerate(HALVES):
+        scan_of(rv(wide, 3 * lo, 3 * n), vw("xi", 3 * lo, 3 * n), vw("pm", 3 * lo, 3 * n), A.mult, A.add)
+        lists = vw("rows", wide + 3 * lo + 2, n, 3)
+        do("a", lambda: g.scalar.activation(ap(vw("lsr", lo, n)), ap(lists), F.Identity, bias=MID), [lists], [vw("lsr", lo, n)])
+        ts(vw("yt", lo, n), ys[i], 1.0, None, A.mult)
+        dma("s", T.y[:, lo:lo + n], ap(vw("yt", lo, n)), "out", 0, [vw("yt", lo, n)], [])
+    dma("a", T.ls[:, :], T.lsr[0:128:8, :], "out", 0, [vw("lsr", 0, C)], [])
     for sem in sorted(total):
         if known["g"].get(sem, 0) < total[sem]:
             g.wait_ge(T.sem[sem], total[sem])

from concourse.bass import DstId, RemoteDMATransfer
from concourse.mybir import dt, AluOpType, ActivationFunctionType

C = 384
HALF = C // 2
STEPS = [1, 2, 3]
KT = C // 16
PAD = 16
ROWS = 37
SLOTS = 16
TABS = 20
BIG, LIFT, MID = 2048.0, 512.0, 192.0
TINY = 2.0 ** -100
OPT = {}

SCRATCH = {
    "ut": ("sbuf", [128, 512], "bfloat16"), "qu": ("sbuf", [128, 128], "float8_e4m3fn_x4"), "qus": ("sbuf", [128, 128], "uint8"),
    "qr": ("sbuf", [128, 128], "float8_e4m3fn_x4"), "qrs": ("sbuf", [128, 128], "uint8"),
    "vt": ("sbuf", [128, 512], "bfloat16"), "qv": ("sbuf", [128, 128], "float8_e4m3fn_x4"), "qvs": ("sbuf", [128, 128], "uint8"),
    "wq": ("sbuf", [128, 512], "float8_e4m3fn_x4"), "wp": ("sbuf", [128, 512], "uint8"),
    "ones": ("sbuf", [128, 528], "bfloat16"), "et": ("sbuf", [128, 528], "bfloat16"),
    "qe": ("sbuf", [128, 512], "float8_e4m3fn_x4"), "qes": ("sbuf", [128, 512], "uint8"),
    "lai": ("sbuf", [128, KT], "int32"), "lbi": ("sbuf", [128, KT], "int32"),
    "im": ("sbuf", [128, 48], "int32"), "im2": ("sbuf", [128, 48], "int32"), "ma": ("sbuf", [128, 48], "bfloat16"), "mb": ("sbuf", [128, 48], "bfloat16"),
    "et8": ("sbuf", [128, 528], "bfloat16"), "qe8": ("sbuf", [128, 256], "float8_e4m3fn_x4"), "qe8s": ("sbuf", [128, 256], "uint8"),
    "mask": ("sbuf", [128, C], "bfloat16"), "ik": ("sbuf", [128, KT], "int32"), "ip": ("sbuf", [128, 8], "int32"),
    "cols": ("sbuf", [128, 16], "float32"), "plist": ("sbuf", [128, 8], "uint16"),
    "xi": ("sbuf", [128, 3 * C], "bfloat16"), "pm": ("sbuf", [128, 3 * C], "float16"),
    "num": ("sbuf", [128, 2 * C], "float32"), "lsr": ("sbuf", [128, C], "float32"), "yt": ("sbuf", [128, C], "float32"),
    "rows": ("sbuf", [128, C * (3 * ROWS + 1)], "bfloat16"), "sc": ("sbuf", [128, C * SLOTS], "float16"),
    "tf": ("sbuf", [128, KT * 3 * TABS], "float32"), "tu": ("sbuf", [128, KT * 3 * SLOTS], "uint16"),
    "big": ("sbuf", [128, 2 * C], "bfloat16"),
    "te": ("sbuf", [128, 2 * KT], "float32"), "zb": ("sbuf", [128, 8 * C], "bfloat16"), "alt": ("sbuf", [128, 2 * C], "bfloat16"),
}
for r in range(4):
    SCRATCH["xt%d" % r] = ("sbuf", [128, 4 * C], "bfloat16")
    SCRATCH["q%d" % r] = ("sbuf", [128, C], "float8_e4m3fn_x4")
    SCRATCH["qs%d" % r] = ("sbuf", [128, C], "uint8")
for r in range(3):
    for k in ("f", "h", "o"):
        SCRATCH["%s%d" % (k, r)] = ("sbuf", [128, 4 * C], "bfloat16")
    SCRATCH["zt%d" % r] = ("sbuf", [128, PAD + 4 * C], "bfloat16")
    for k in ("lq", "zq"):
        SCRATCH["%s%d" % (k, r)] = ("sbuf", [128, C], "float8_e4m3fn_x4")
    for k in ("lp", "zp"):
        SCRATCH["%s%d" % (k, r)] = ("sbuf", [128, C], "uint8")
    SCRATCH["t1l%d" % r] = ("sbuf", [128, KT], "uint16")
    SCRATCH["t2l%d" % r] = ("sbuf", [128, 2 * KT], "uint16")
    for k in ("sf", "sr"):
        SCRATCH["%s%d" % (k, r)] = ("sbuf", [128, C], "float32")
for k in ("fd", "za", "zad", "zi", "zbd"):
    SCRATCH[k] = ("sbuf", [128, 4 * C], "bfloat16")
for r in range(8):
    SCRATCH["pb%d" % r] = ("psum", [128, 512], "float32")
SEMAPHORES = ["cv", "ca", "cp", "cg", "dx0", "dx1", "du", "dl", "dw", "dv", "sent", "out"] + ["%s%d" % (k, r) for k in ("aq", "at", "au", "av") for r in range(3)]


def rank_program(g, core, T, topo):
    me = T.rank_of(core)
    if me is None:
        return
    n_ranks = len(T.cores)
    A, F = AluOpType, ActivationFunctionType
    queues = {"v": g.vector, "a": g.scalar, "p": g.tensor, "g": g, "s": g.sync}
    own = {"v": "cv", "a": "ca", "p": "cp", "g": "cg"}
    total = {}
    known = {q: {} for q in queues}
    log = {}

    def vw(name, a, n, step=1):
        return (name, a, a + n * step, step)

    def ap(v):
        name, a, b, st = v
        return T[name][:, a:b] if st == 1 else T[name][:, a:b - st + 1:st]

    def wait(q, tok):
        sem, n, clock = tok
        if known[q].get(sem, 0) >= n:
            return
        queues[q].wait_ge(T.sem[sem], n)
        known[q][sem] = n
        for k in clock:
            if clock[k] > known[q].get(k, 0):
                known[q][k] = clock[k]

    def order(q, kind, reads, writes):
        deps = {}
        for v, w in [(v, False) for v in reads] + [(v, True) for v in writes]:
            name, a, b, st = v
            bank = SCRATCH[name][0] == "psum"
            for a2, b2, st2, w2, k2, tok in log.get(name, ()):
                if k2 == kind and kind != "dma" and not (w2 and not w):
                    continue
                if not bank and (b2 - st2 < a or b - st < a2 or not (w or w2) or (st == st2 and st > 1 and (a - a2) % st)):
                    continue
                if tok[0] not in deps or deps[tok[0]][1] < tok[1]:
                    deps[tok[0]] = tok
        for sem in sorted(deps, key=lambda s: s == own.get(q)):
            wait(q, deps[sem])

    def note(kind, reads, writes, tok):
        for v, w in [(v, False) for v in reads] + [(v, True) for v in writes]:
            log.setdefault(v[0], []).append((v[1], v[2], v[3], w, kind, tok))

    def do(q, make, reads, writes):
        order(q, q, reads, writes)
        sem = own[q]
        total[sem] = total.get(sem, 0) + 1
        make().then_inc(T.sem[sem], 1)
        note(q, reads, writes, (sem, total[sem], dict(known[q])))

    def dma(q, out, in_, sem, full, reads, writes):
        order(q, "dma", reads, writes)
        total[sem] = total.get(sem, 0) + 16
        queues[q].dma_start(out, in_).then_inc(T.sem[sem], 16)
        note("dma", reads, writes, (sem, full, dict(known[q])))

    def ts(out, in0, s1, s2, op0, op1=None):
        rd = [in0] + [s for s in (s1, s2) if isinstance(s, tuple)]
        x1, x2 = [ap(s) if isinstance(s, tuple) else s for s in (s1, s2)]
        if op1 is None:
            do("v", lambda: g.vector.tensor_scalar(ap(out), ap(in0), x1, None, op0), rd, [out])
        else:
            do("v", lambda: g.vector.tensor_scalar(ap(out), ap(in0), x1, x2, op0, op1), rd, [out])

    def tt(out, in0, in1, op, off=None):
        src = ap(in0).indirect(ap(off)) if off else ap(in0)
        do("v", lambda: g.vector.tensor_tensor(ap(out), src, ap(in1), op), [in0, in1] + ([off] if off else []), [out])

    def tcopy(out, in_):
        do("v", lambda: g.vector.tensor_copy(ap(out), ap(in_)), [in_], [out])

    def act(out, in_, scale=1.0):
        if scale == 1.0:
            do("a", lambda: g.scalar.activation(ap(out), ap(in_), F.Copy), [in_], [out])
        else:
            do("a", lambda: g.scalar.activation(ap(out), ap(in_), F.Copy, scale=scale), [in_], [out])

    def copy_on(q, out, in_):
        if q == "a":
            return act(out, in_)
        if q == "v":
            return tcopy(out, in_)
        do("g", lambda: g.affine_select(ap(out), ap(in_), [[0, (in_[2] - in_[1]) // in_[3]]], A.is_gt, 0.0, 1, 0), [in_], [out])

    def gather(q, out, win, off, scale=None):
        if q == "v":
            do("v", lambda: g.vector.tensor_copy(ap(out), ap(win).indirect(ap(off))), [win, off], [out])
        elif scale:
            do("a", lambda: g.scalar.activation(ap(out), ap(win).indirect(ap(off)), F.Copy, scale=scale), [win, off], [out])
        else:
            do("a", lambda: g.scalar.activation(ap(out), ap(win).indirect(ap(off)), F.Copy), [win, off], [out])

    def quant(q, s, tile, a, n, at=None):
        t = vw(tile, 4 * a if at is None else at, 4 * n)
        do("v", lambda: g.vector.quantize_mx(ap(vw(q, a, n)), ap(vw(s, a, n)), ap(t)), [t], [vw(q, a, n), vw(s, a, n)])

    def mm(bank, lq, ls, la, rq, rs, ra, n):
        o = vw("pb%d" % bank, 0, n)
        rd = [vw(lq, la, 128), vw(ls, la, 128), vw(rq, ra, n), vw(rs, ra, n)]
        do("p", lambda: g.tensor.matmul_mx(ap(o), ap(rd[0]), ap(rd[1]), ap(rd[2]), ap(rd[3]), True, True), rd, [o])
        return o

    def send(dst, out, in_, sem, codes=False):
        order("g", "g", [in_], [])
        rid, pid = topo.addr(dst)[:2]
        o, i = (ap(out).bitcast(dt.uint8), ap(in_).bitcast(dt.uint8)) if codes else (ap(out), ap(in_))
        g.remote_dma(o, i, T.sem[sem], T.sem.sent, pid, rid, topo.mask(core, dst))
        total["sent"] = total.get("sent", 0) + len(topo.engines(core, dst))

    nxt = {}

    def place(buf, n):
        a = nxt.get(buf, 0)
        nxt[buf] = a + n
        return a

    def row():
        return place("rows", C)

    def rv(a, lo=0, n=C):
        return vw("rows", a + lo, n)

    def tab():
        return vw("tf", place("tf", KT), KT)

    def off(n=KT):
        return vw("tu", place("tu", n), n)

    def part(o, lo, n):
        return (o[0], o[1] + lo, o[1] + lo + n, 1)

    def cols_of(t, lo, n):
        return part(t, lo // 16, n // 16)

    mask = "mask"

    def scan_of(o, d0, d1, op0, op1):
        do("v", lambda: g.vector.tensor_tensor_scan(ap(o), ap(d0), ap(d1), 0.0, op0, op1), [d0, d1], [o])

    def scan(out, a, lo=0, n=C):
        scan_of(vw("sc", out + lo, n), vw(mask, lo, n), a if isinstance(a, tuple) else rv(a, lo, n), A.add, A.max)

    def picked(s, lo=0, n=C):
        return vw("sc", s + lo + 15, n // 16, 16)

    col = {k: vw("cols", i, 1) for i, k in enumerate(("p15", "z", "k", "turn", "one_2k", "third", "odd", "sign"))}

    def turn(o, s, lo=0, n=C):
        ts(cols_of(o, lo, n), picked(s, lo, n), col["turn"], None, A.add)

    def run(steps, n=99):
        for _ in range(min(n, len(steps))):
            steps.pop(0)()

    dma("a", T.lai[:, :], T.la[:, :], "dl", 32, [], [vw("lai", 0, KT)])
    dma("s", T.lbi[:, :], T.lb[:, :], "dl", 32, [], [vw("lbi", 0, KT)])
    dma("a", T.ut[:, :], T.u[:, :], "du", 16, [], [vw("ut", 0, 512)])
    dma("s", T.xt0[:, 0:2 * C], T.x[:, 0:2 * C], "dx0", 16, [], [vw("xt0", 0, 2 * C)])
    dma("s", T.xt0[:, 2 * C:4 * C], T.x[:, 2 * C:4 * C], "dx1", 16, [], [vw("xt0", 2 * C, 2 * C)])

    W = 48
    do("g", lambda: g.iota(T.im[:, :], [[1, W]], 128, -1), [], [vw("im", 0, W)])
    do("g", lambda: g.iota(T.ip[:, :], [[16, 8]], 0, 0), [], [vw("ip", 0, 8)])
    do("g", lambda: g.iota(T.num[:, :], [[1, 2 * C]], -C, 0, allow_small_or_imprecise_dtypes=True), [], [vw("num", 0, 2 * C)])
    def fill(v, x):
        do("v", lambda: g.vector.memset(ap(v), x), [], [v])

    fill(vw("ones", 0, 528), 1.0)
    do("g", lambda: g.affine_select(T.et[:, :], T.ones[:, :], [[-1, 528]], A.is_equal, 0.0, 8, 4), [vw("ones", 0, 528)], [vw("et", 0, 528)])
    do("g", lambda: g.iota(T.ik[:, :], [[16, KT]], 0, 0), [], [vw("ik", 0, KT)])
    ident = row()
    im2 = vw("im2", 0, W)
    first = vw("im2", 0, 1)
    fill(vw("xi", 0, C, 3), 0.0)
    ts(im2, vw("im", 0, W), 15, None, A.bitwise_and)
    fill(vw("xi", 1, C, 3), 0.0)
    ts(vw("ma", 0, W), im2, 0, -BIG, A.is_equal, A.mult)
    ts(vw("mb", 0, W), im2, 1, LIFT, A.is_equal, A.mult)
    ts(col["k"], first, 1, LIFT, A.not_equal, A.mult)
    tcopy(vw("pm", 0, C, 3), vw("xi", 0, C, 3))
    tt(vw(mask, 0, W), vw("ma", 0, W), vw("mb", 0, W), A.add)
    ts(col["turn"], col["k"], -1.0, MID, A.mult, A.add)
    tcopy(vw("plist", 0, 8), vw("ip", 0, 8))
    ts(col["z"], first, 0, 16, A.not_equal, A.mult)
    tcopy(vw(mask, W, W), vw(mask, 0, W))
    num_t, low_t, gap, both_l = tab(), tab(), tab(), tab()
    o_gap, o_sum = off(), off()

    def spread(o, at, scale):
        gather("a", vw("pm", at, C, 3), vw("num", 0, 2 * C), o, scale)

    tt(gap, vw("lai", 0, KT), vw("lbi", 0, KT), A.subtract)
    tt(both_l, vw("lai", 0, KT), vw("lbi", 0, KT), A.add)
    tcopy(vw(mask, 2 * W, 2 * W), vw(mask, 0, 2 * W))
    ts(col["third"], col["turn"], 3.0, 2.0, A.mult, A.add)
    ts(o_gap, gap, float(C), None, A.add)
    tcopy(o_sum, both_l)
    tcopy(vw(mask, 4 * W, 4 * W), vw(mask, 0, 4 * W))
    spread(o_gap, 1, 0.5)
    quant("qu", "qus", "ut", 0, 128)
    tt(col["p15"], col["z"], first, A.subtract)
    ts(col["one_2k"], col["k"], 2.0, 1.0, A.mult, A.add)
    ts(col["odd"], col["turn"], 2.0, 1.0, A.mult, A.add)
    ts(col["sign"], first, -0.25, 1.0, A.mult, A.add)
    do("v", lambda: g.vector.tensor_copy(T.qr[:, :].bitcast(dt.uint32), T.qu[:, :].bitcast(dt.uint32).indirect(T.plist[:, 0:8])), [vw("qu", 0, 128), vw("plist", 0, 8)], [vw("qr", 0, 128)])
    do("a", lambda: g.scalar.activation(T.qrs[:, :], T.qus[:, :].indirect(T.plist[:, 0:8]), F.Copy), [vw("qus", 0, 128), vw("plist", 0, 8)], [vw("qrs", 0, 128)])
    spread(o_sum, 2, 0.5)
    fill(vw("te", 0, 2 * KT), 0.0)
    fill(vw("big", 0, C, 2), BIG)
    fill(vw("big", 1, C, 2), 0.0)

    HALVES = ((0, HALF), (HALF, HALF))
    THIRDS = ((0, 128), (128, 128), (256, 128))
    PIECES = ((0, 256), (256, 128))
    around = [[], [], []]

    def exchange(flags, gap):
        s, flip, gap2 = place("sc", C), tab(), tab()
        return [lambda i=i, lo=lo, n=n: scan(s, flags[i], lo, n) for i, (lo, n) in enumerate(HALVES)] + [
            lambda: ts(flip, picked(s), -2.0, col["one_2k"], A.mult, A.add), lambda: tt(gap2, gap, flip, A.mult)], gap2

    for r, d in enumerate(STEPS):
        last = r == len(STEPS) - 1
        dst = T.cores[(me + d) % n_ranks]
        q, qs, xt = "q%d" % r, "qs%d" % r, "xt%d" % r
        lq, lp, t1l, t2l = "lq%d" % r, "lp%d" % r, "t1l%d" % r, "t2l%d" % r
        src = T.cores[(me - d) % n_ranks]
        ne = len(topo.engines(src, core))
        total["aq%d" % r], total["at%d" % r], total["au%d" % r], total["av%d" % r] = (2 + (r == 0)) * ne, ne, ne, ne
        note("dma", [], [vw(lq, 0, C), vw(lp, 0, C)], ("aq%d" % r, total["aq%d" % r], {}))
        got1, got2, got4 = vw(t1l, 0, KT), vw(t2l, 0, KT), vw(t2l, KT, KT)
        for t, sem in ((got1, "at"), (got2, "au"), (got4, "av")):
            note("dma", [], [t], ("%s%d" % (sem, r), ne, {}))
        f, zt, h, o = ["%s%d" % (k, r) for k in ("f", "zt", "h", "o")]
        fd, za, zad, zb, zbd, hg = "fd", "za", "zad", "zb", "zbd", "zbd"
        sf, sr = "sf%d" % r, "sr%d" % r
        nxt["sc"] = 0
        held, free = ((0, 7), (1, 2))[r % 2], ((1, 2), (0, 7))[r % 2]

        def plane(t, b, lo=0, n=C):
            return vw(t, C * b + lo, n)

        sv = []
        for i in range(2):
            run(around[i])
            quant(q, qs, xt, HALF * i, HALF)
            sv.append(mm(held[i], "qr", "qrs", 0, q, qs, HALF * i, HALF))
            if r == 0:
                send(dst, vw(lq, HALF * i, HALF), vw(q, HALF * i, HALF), "aq0", True)
        run(around[2])
        if r > 0:
            send(dst, vw(lq, 0, C), vw(q, 0, C), "aq%d" % r, True)
        send(dst, vw(lp, 0, C), vw(qs, 0, C), "aq%d" % r)
        if r == 0:
            wait("s", ("aq0", total["aq0"], {}))
            dma("s", T.wq[:, :].bitcast(dt.uint8), T.wc[:, :], "dw", 32, [], [vw("wq", 0, 512)])
            dma("s", T.wp[:, :], T.ws[:, :], "dw", 32, [], [vw("wp", 0, 512)])
            dma("s", T.vt[:, :], T.v[:, :], "dv", 16, [], [vw("vt", 0, 512)])
            do("g", lambda: g.iota(ap(rv(ident)), [[1, C]], -int(MID), 0, allow_small_or_imprecise_dtypes=True), [], [rv(ident)])
            for b in range(4):
                quant("qe", "qes", "et", 128 * b, 128, 8 - b)
        own_f = [mm(5 + b, "qe", "qes", 128 * b, q, qs, 0, C) for b in range(2)]
        wide, twin, p_s, t_k = place("rows", 3 * C), place("rows", 2 * C), place("sc", C), off()
        chosen = [vw("rows", wide + 3 * lo + 2, n, 3) for lo, n in HALVES]
        for i, (lo, n) in enumerate(HALVES):
            side = vw("xi", 3 * lo + 2, n, 3)
            do("a", lambda: g.scalar.activation(ap(side), ap(sv[i]), F.Sign, bias=TINY), [sv[i]], [side])
        if r == 0:
            act(vw("et8", 0, 528), vw("et", 0, 528), 0.125)
        for i, (lo, n) in enumerate(HALVES):
            act(vw(sf, lo, n), sv[i])
        choose = [lambda lo=lo, n=n: scan_of(rv(wide, 3 * lo, 3 * n), vw("xi", 3 * lo, 3 * n), vw("pm", 3 * lo, 3 * n), A.mult, A.add) for lo, n in HALVES]
        diag = [lambda i=i, lo=lo, n=n: scan(p_s, chosen[i], lo, n) for i, (lo, n) in enumerate(HALVES)]
        copy = [lambda i=i, lo=lo, n=n: tcopy(vw("rows", twin + 2 * lo, n, 2), chosen[i]) for i, (lo, n) in enumerate(HALVES)]
        offs = [lambda lo=lo, n=n: ts(cols_of(t_k, lo, n), picked(p_s, lo, n), 3.0, col["third"], A.mult, A.add) for lo, n in HALVES]
        if r > 0:
            run([choose[0], diag[0], choose[1], offs[0], copy[0], diag[1], copy[1], offs[1]])
        else:
            run([choose[0], choose[1], diag[0], copy[0], diag[1], offs[0], copy[1], offs[1]])
            for b in range(2):
                quant("qe8", "qe8s", "et8", 128 * b, 128, 6 - b)
            ts(num_t, vw("ik", 0, KT), col["p15"], None, A.add)
        pair = place("tf", 2 * KT)
        to_self, p_t = vw("tf", pair, KT, 2), vw("tf", pair + 1, KT, 2)

        def unpack_own(k):
            b, lo = k // 2, HALF * (k % 2)
            act(plane(o, b, lo, HALF), part(own_f[b], lo, HALF))
            if k in (1, 3):
                b2 = 2 + k // 2
                own_f.append(mm(3 + b2, "qe", "qes", 128 * b2, q, qs, 0, C))

        fp = []

        def unpack_src(b, out, lo, n):
            if len(fp) == b:
                e, es, ea = ("qe", "qes", 128 * b) if b < 2 else ("qe8", "qe8s", 128 * (b - 2))
                fp.append(mm((free + (3, 4))[b], e, es, ea, lq, lp, 0, C))
            act(plane(out, b, lo, n), part(fp[b], lo, n), 0.125 if b < 2 else 1.0)

        spare = [lambda k=k: unpack_own(k) for k in (0, 1, 2, 3, 4, 6)]

        low, twin2, ss, t2 = place("rows", 2 * C), row(), place("sc", C), off()
        for lo, n in HALVES:
            gather("a", vw("rows", twin + 2 * lo + 1, n, 2), rv(wide, 0, 3 * C), cols_of(t_k, lo, n))
        run(spare, 1)
        for i, (lo, n) in enumerate(HALVES):
            scan(ss, vw("rows", twin + 2 * lo + 1, n, 2), lo, n)
            scan_of(rv(low, 2 * lo, 2 * n), vw("big", 2 * lo, 2 * n), rv(twin, 2 * lo, 2 * n), A.add, A.min)
            copy_on("g", rv(twin2, 128 * i, 128), vw("rows", low + 256 * i + 1, 128, 2))
            ts(cols_of(t2, lo, n), picked(ss, lo, n), 2.0, col["odd"], A.mult, A.add)
        if r == 0:
            ts(low_t, num_t, -MID, col["k"], A.add, A.add)
        behind = [lambda a=twin2, b=low: copy_on("a", rv(a, 256, 128), vw("rows", b + 513, 128, 2))]
        at, low, twin, t_k = rv(twin, 0, 2 * C), rv(low, 0, 2 * C), twin2, t2
        cut = THIRDS if OPT.get("p3") else HALVES
        for k in range(1, 7):
            at2, low2, twin2, t2 = row(), row(), row(), off()
            ss = place("sc", C)

            def lower(j):
                lo, n = THIRDS[j]
                tt(rv(low2, lo, n), low, rv(twin, lo, n), A.min, cols_of(t_k, lo, n))
                if j == 0 or j == 1 and k < 6:
                    copy_on("g", rv(twin2, lo, n), rv(low2, lo, n))
                else:
                    behind.append(lambda a=twin2, b=low2: copy_on("a", rv(a, lo, n), rv(b, lo, n)))

            for lo, n in cut:
                gather("a", rv(at2, lo, n), at, cols_of(t_k, lo, n))
            run(behind, 1)
            run(spare, 1)
            plan = OPT.get("p3", "s0 l0 t0 s1 l1 t1 l2") if k else OPT.get("p30", "l0 s0 l1 t0 s1 l2 t1")
            if k == 6:
                plan = OPT.get("p36", plan)
            for w in plan.split():
                j = int(w[1])
                if w[0] == "l":
                    lower(j)
                elif w[0] == "s":
                    scan(ss, at2, *cut[j])
                else:
                    turn(t2, ss, *cut[j])
            at, low, twin, t_k = rv(at2), rv(low2), twin2, t2
        far, m, at2, t2, ss, s = row(), row(), row(), off(8), place("sc", 128), place("sc", C)
        both, tears = place("tf", 2 * KT), off()

        def farther(j):
            lo, n = THIRDS[j]
            tt(rv(far, lo, n), low, rv(twin, lo, n), A.min, cols_of(t_k, lo, n))

        def lowest(j):
            lo, n = THIRDS[j]
            tt(rv(m, lo, n), rv(far), part(low, lo, n), A.min, cols_of(t_k, lo, n))

        gather("a", rv(at2, 0, 128), at, cols_of(t_k, 0, 128))
        run(behind)
        unpack_src(0, f, 0, C)
        copy_on("g", plane(fd, 0), plane(f, 0))
        for b in range(1, 4):
            unpack_src(b, f, 0, C)
        unpack_src(1, fd, 0, C)
        calls = {"p": lambda: ts(p_t, picked(p_s), col["turn"], None, A.add), "q": lambda: tt(to_self, num_t, p_t, A.subtract),
                 "s": lambda: scan(ss, at2, 0, 128), "t": lambda: turn(t2, ss, 0, 128), "f0": lambda: farther(0), "f1": lambda: farther(1), "f2": lambda: farther(2),
                 "m0": lambda: tt(rv(m, 0, 128), low, rv(far, 0, 128), A.min, t2), "m1": lambda: lowest(1), "m2": lambda: lowest(2),
                 "d0": lambda: scan(s, m, 0, 128), "d1": lambda: scan(s, far, 128, 128), "d2": lambda: scan(s, part(low, 256, 128), 256, 128),
                 "e": lambda: tt(vw("te", 1, KT, 2), picked(s), low_t, A.is_equal),
                 "x": lambda: scan_of(vw("tf", both, 2 * KT), vw("te", 0, 2 * KT), vw("tf", pair, 2 * KT), A.mult, A.add),
                 "c": lambda: tcopy(tears, vw("tf", both + 1, KT, 2))}
        if r == 0:
            steps = [lambda: fill(vw("alt", 0, C, 2), 0.0), lambda: fill(vw("alt", 1, C, 2), 1.0)]
        else:
            steps, gap = exchange([vw("xi", 3 * lo + 1, n, 3) for lo, n in HALVES], gap)
            o_gap = off()
            steps.append(lambda: ts(o_gap, gap, float(C), None, A.add))
        calls["+"] = lambda: run(steps, 1)
        for w in OPT.get("end", "p s + f0 t f1 m0 d2 d1 q d0 f2 e + x m1 c").split():
            calls[w]()
        send(dst, got1, tears, "at%d" % r)

        lead = [m, row(), row(), row()]

        def follow(j):
            gather("a", rv(lead[j + 1]), rv(lead[j]), t_k)

        tr, tr2, tr4 = row(), row(), row()
        jump2, jump4 = off(), off()
        run(steps, 1)
        for j, (out, win) in enumerate(((tr, ident), (tr2, tr))):
            for qq, (lo, n) in zip("va", HALVES):
                gather(qq, rv(out, lo, n), rv(win), cols_of(tears, lo, n))
            if j == 0:
                lowest(2)
        run(steps, 1)
        s = place("sc", C)
        scan(s, tr2)
        run(steps)
        turn(jump2, s)
        send(dst, got2, jump2, "au%d" % r)

        def z1(b):
            if b < 2:
                tt(plane(za, b), plane(f, b), plane(fd, b), A.add, got1)
            else:
                tt(plane(za, b), fp[b], plane(fd, b), A.add)

        shared = OPT.get("shared", (2, 3))

        def z2(b):
            if b not in shared:
                tt(vw(zb, 2 * C * b + 1, C, 2), plane(za, b), plane(zad, b), A.add, got2)
            else:
                scan_of(vw(zb, 2 * C * b, 2 * C), vw("alt", 0, 2 * C), vw("zi", 2 * C * (b - 2), 2 * C), A.mult, A.add)

        def z3(b, lo=0, n=C):
            tt(vw(zt, 4 * lo + b, n, 4), vw(zb, 2 * C * b, 2 * C), plane(zbd, b, lo, n), A.add, cols_of(got4, lo, n))

        def beside(qq, b):
            copy_on(qq, vw("zi", 2 * C * (b - 2), C, 2) if b in shared else plane(zad, b), plane(za, b))

        s4, sp = place("sc", C), 256
        calls = {"f": follow, "g": lambda b: gather("a", plane(fd, b), plane(f, b), got1), "t": lambda b: gather("a", rv(tr4), rv(tr2), jump2),
                 "z": z1, "y": z2, "x": z3, "a": lambda b: beside("a", b), "b": lambda b: beside("g", b),
                 "c": lambda b: copy_on("a", plane(zbd, b), vw(zb, 2 * C * b + 1, C, 2)), "d": lambda b: copy_on("g", plane(zbd, b), vw(zb, 2 * C * b + 1, C, 2)),
                 "e": lambda b: gather("a", vw("zi", 2 * C * (b - 2) + 1, C, 2), plane(za, b), got2) if b in shared else None,
                 "B": lambda b: copy_on("g", plane(zad, b, 0, sp), plane(za, b, 0, sp)), "h": lambda b: copy_on("a", plane(zad, b, sp, C - sp), plane(za, b, sp, C - sp)),
                 "D": lambda b: copy_on("g", plane(zbd, b, 0, sp), vw(zb, 2 * C * b + 1, sp, 2)), "i": lambda b: copy_on("a", plane(zbd, b, sp, C - sp), vw(zb, 2 * C * b + 1 + 2 * sp, C - sp, 2)),
                 "s": lambda b: scan(s4, tr4), "p": lambda b: (spread(o_gap, 1, 0.5) if r else None) if b else act(vw("pm", 0, C, 3), vw("pm", 1, C, 3), -2.0),
                 "u": lambda b: (ts(jump4, picked(s4), 2.0, col["odd"], A.mult, A.add), send(dst, got4, jump4, "av%d" % r))}
        for w in OPT.get("zplan", "f0 g2 t0 g3 z0 b0 z1 B1 z2 a2 e2 h1 s0 u0 z3 a3 e3 y0 d0 y1 c1 y2 D2 i2 y3 c3 f1 f2 p1 p0 x0 x1 x2").split():
            calls[w[0]](int(w[1]))
        zq, zp = "zq%d" % r, "zp%d" % r

        def layer(bank, b, lo, n):
            act(plane(h, b, lo, n), mm(bank, "wq", "wp", 128 * b, zq, zp, lo, n), 0.03125)

        z3(3, 0, 256)
        z3(3, 256, 128)
        for i, (lo, n) in enumerate(THIRDS):
            quant(zq, zp, zt, lo, n)
            layer((free[0], free[1], 3)[i], 0, lo, n)
        for i, (lo, n) in enumerate(HALVES):
            layer((4, free[0])[i], 1, lo, n)
        layer(free[1], 2, 0, C)
        layer(3, 3, 0, C)
        s, t_r = place("sc", C), off()
        scan(s, lead[3])
        if r == 0:
            quant("qv", "qvs", "vt", 0, 128)
        if last:
            ts(vw("xi", 2, C, 3), vw("xi", 0, C, 3), col["sign"], None, A.add)
        turn(t_r, s)

        x2 = "xt%d" % (r + 1)
        for b in (2, 3):
            gather("a", plane(hg, b, HALF, HALF), plane(h, b), cols_of(tears, HALF, HALF))
        for lo, n in HALVES:
            gather("a", vw(sr, lo, n), vw(sf, 0, C), cols_of(t_r, lo, n))

        def state(b, lo=0, n=C, x2=x2, h=h, o=o, tears=tears, kept=own_f):
            if b >= 2 and lo == HALF:
                tt(vw(x2, 4 * lo + b, n, 4), part(kept[b], lo, n), plane(hg, b, lo, n), A.add)
            else:
                tt(vw(x2, 4 * lo + b, n, 4), plane(h, b), plane(o, b, lo, n), A.add, cols_of(tears, lo, n))

        compare = [lambda i=i, lo=lo, n=n, sv=sv, sr=sr: tt(vw("xi", 3 * lo + 1, n, 3), sv[i], vw(sr, lo, n), A.is_lt) for i, (lo, n) in enumerate(HALVES)]
        state(0)
        state(1)
        state(2, 0, HALF)
        state(3, 0, HALF)
        around = [[lambda: state(2, HALF, HALF)], [lambda: state(3, HALF, HALF), compare[0]], [compare[1]]]
    q, qs = "q3", "qs3"
    ys = []
    for i, (lo, n) in enumerate(HALVES):
        run(around[i])
        quant(q, qs, x2, lo, n)
        ys.append(mm(free[i], "qv", "qvs", 0, q, qs, lo, n))
        dma("s", T.oc[:, 4 * lo:4 * lo + 4 * n], ap(vw(q, lo, n)).bitcast(dt.uint8), "out", 0, [vw(q, lo, n)], [])
    for k in range(4):
        dma("saaa"[k], T.osc[4 * k:4 * k + 4, :], T[qs][32 * k:32 * k + 4, :], "out", 0, [vw(qs, 0, C)], [])
    run(around[2])
    wide = place("rows", 3 * C)
    for i, (lo, n) in enumerate(HALVES):
        scan_of(rv(wide, 3 * lo, 3 * n), vw("xi", 3 * lo, 3 * n), vw("pm", 3 * lo, 3 * n), A.mult, A.add)
        lists = vw("rows", wide + 3 * lo + 2, n, 3)
        do("a", lambda: g.scalar.activation(ap(vw("lsr", lo, n)), ap(lists), F.Identity, bias=MID), [lists], [vw("lsr", lo, n)])
        ts(vw("yt", lo, n), ys[i], 1.0, None, A.mult)
        dma("s", T.y[:, lo:lo + n], ap(vw("yt", lo, n)), "out", 0, [vw("yt", lo, n)], [])
    dma("a", T.ls[:, :], T.lsr[0:128:8, :], "out", 0, [vw("lsr", 0, C)], [])
    for sem in sorted(total):
        if known["g"].get(sem, 0) < total[sem]:
            g.wait_ge(T.sem[sem], total[sem])
